import numpy as np, ml_dtypes
CORES = [23,119,17,113]
N = 4
import mx_ref
BF = ml_dtypes.bfloat16
def gentries(a):
    return np.ascontiguousarray(a.reshape(8, 16, -1).transpose(0, 2, 1)).reshape(8, -1)
def gtable(e):
    e = np.asarray(e); return np.ascontiguousarray(e.reshape(8, -1, 16).transpose(0, 2, 1)).reshape(128, -1).astype(np.int32)
def gcols(t, e):
    v = np.concatenate([t.reshape(8, 16, -1, 4), np.zeros((8, 16, 1, 4), BF)], axis=2)
    return np.ascontiguousarray(np.stack([v[g][:, e[g]] for g in range(8)])).reshape(128, -1)
def tile(rs):
    return np.stack(rs, axis=2).reshape(128, -1).astype(BF)
def cut(t, i, w=512):
    return t[:, w * i:w * i + w]
def pick(q, e):
    c = np.concatenate([q[0].reshape(128, -1, 4), np.zeros((128, 1, 4), np.uint8)], axis=1); s = np.concatenate([q[1], np.ones((16, 1), np.uint8)], axis=1)
    return (np.ascontiguousarray(c[:, e].reshape(128, -1)), np.ascontiguousarray(s[:, e]))
def join(*qs):
    return (np.concatenate([q[0] for q in qs], axis=1), np.concatenate([q[1] for q in qs], axis=1))
def put(q, e, v):
    c, s = q[0].reshape(128, -1, 4).copy(), q[1].copy(); c[:, e] = v[0].reshape(128, -1, 4); s[:, e] = v[1]
    return (c.reshape(128, -1), s)
def pk(c, s):
    return (np.ascontiguousarray(c), mx_ref.live(s))
def emit(q):
    return q[0], q[1]
def packed(v, rng):
    q = [mx_ref.quantize(np.ascontiguousarray(v[r])) for r in range(N)]
    return np.stack([a for a, b in q]), np.stack([mx_ref.plane(b, rng) for a, b in q])
def values_of_codes():
    e, c = np.zeros((128, 128, 4), np.float32), np.zeros((128, 2, 4), np.uint8)
    e[np.arange(128), np.arange(128), 0] = 1
    c[:127, :, 0] = np.arange(256).reshape(2, 128).T[:127]
    return mx_ref.matmul(mx_ref.quantize(e.reshape(128, 512).astype(BF)), (c.reshape(128, 8), np.full((16, 2), 127, np.uint8))).T.reshape(-1).astype(np.float64)
CODE_VALUE, SCALE_VALUE = values_of_codes(), 2.0 ** (np.arange(256) - 127.0)
def decode(q):
    return (CODE_VALUE[q[0]].reshape(16, 8, -1, 4) * SCALE_VALUE[q[1]][:, None, :, None] + 0.0).reshape(128, -1).astype(np.float32)
def f(rng, *shape):
    return mx_ref.flush((rng.standard_normal(shape, dtype=np.float32) * np.exp2(rng.integers(-2, 3, shape[:-1] + (1,)))).astype(BF))
def wide(rng, *shape, cols=0):
    v = rng.standard_normal(shape, dtype=np.float32) * np.exp2(rng.integers(-12, 13, shape)).astype(np.float32)
    if cols: v *= np.repeat(np.exp2(rng.integers(-cols, cols + 1, shape[:-2] + (1, shape[-1] // 4))) * (rng.random(shape[:-2] + (1, shape[-1] // 4)) > 0.0625), 4, axis=-1).astype(np.float32)
    return mx_ref.flush(v.astype(BF))
C, G, R, L = 448, 256, 3, 2
def big(v, k):
    v = v.astype(np.float32) * np.float32(k)
    v[np.abs(v) < np.float32(2.0 ** -16)] = 0
    return v.astype(BF)
def numbers_of(rng):
    return {"x": big(f(rng, N, 128, 4 * C), 1), "gh": big(f(rng, N, 128, 4 * G), 1), "u": np.array(f(rng, N, 128, 512)), "v": np.array(f(rng, N, 128, 512))}
def weights(rng, w):
    c, p = packed(np.stack([w] * N), rng)
    return {"wc": c, "ws": p}
def still(rng):
    w = np.zeros((128, 4, 128, 4), np.float32)
    i = np.arange(128)
    for b in range(4): w[i, b, i, b] = 32
    return weights(rng, w.reshape(128, 2048).astype(BF))
def matching(rng, n):
    p, i = np.arange(C), rng.permutation(C)[:n]
    h = n // 2
    p[i[:h]] = i[h:2 * h]
    p[i[h:2 * h]] = i[:h]
    return p
def stored(nx, pr):
    return {"nx": np.stack([gtable(nx[r]) for r in range(N)]), "pr": np.stack([gtable(pr[r].reshape(8, R * C)) for r in range(N)])}
def lists_of(rng, same=(), halves=()):
    nx = rng.permuted(np.tile(np.arange(C + G), (N, 8, 1)), axis=2)
    for r in same: nx[r] = nx[r, 0].copy()
    pr = np.stack([matching(rng, C) for i in range(N * 8 * R)]).reshape(N, 8, R, C)
    h = C // 2
    for r in halves:
        for g in range(8):
            for lo, hi in ((0, h), (h, C), (C, C + G)): nx[r, g, lo:hi] = lo + rng.permutation(hi - lo)
            i = h + rng.permutation(h)
            pr[r, g, 0, :h] = i
            pr[r, g, 0, i] = np.arange(h)
    return stored(nx, pr)
def signs(rng):
    return np.stack([rng.permutation(8) % 2 * 2.0 - 1.0 for r in range(N)])
def linked(rng, kind):
    i, a, b, n = rng.permutation(C + G), rng.permutation(C), C + rng.permutation(G), np.arange(C + G)
    if kind == 1: n[i] = np.roll(i, -1)
    if kind == 2:
        n[a] = np.roll(a, -1)
        n[b] = np.roll(b, -1)
    if kind == 3:
        i = np.concatenate([np.stack([a[:G], b], axis=1).reshape(-1), a[G:]])
        n[i] = np.roll(i, -1)
    if kind == 4:
        n[i[::2]] = i[1::2]
        n[i[1::2]] = i[::2]
    if kind == 5: n = np.roll(n, -1)
    if kind == 6: n = np.roll(n, 1)
    if kind == 7: n = i
    return n
def setup_inputs(rng):
    return {**numbers_of(rng), **lists_of(rng), **weights(rng, f(rng, 128, 2048))}
def setup_inputs_ties(rng):
    d = numbers_of(rng)
    c = big(f(rng, 128, 4), 1).astype(np.float32).reshape(8, 16, 4)[:, :8]
    k = np.stack([rng.permutation(C + G) % 2 for r in range(N)])
    k[rng.integers(N)] = 1
    a = np.where(k[:, None, None, :, None] == 1, c[None, :, :, None, :], np.float32(0.0)).astype(BF)
    d["x"].reshape(N, 8, 16, C, 4)[:, :, :8] = a[:, :, :, :C]
    d["gh"].reshape(N, 8, 16, G, 4)[:, :, :8] = a[:, :, :, C:]
    keep = np.zeros((8, 16, 8), bool)
    for g in range(8): keep[g, :8, g] = True
    u = d["u"].reshape(N, 8, 16, 128, 4)
    a = u[:, :, :, ::16].astype(np.float32)
    a[:, ~keep] = 0
    u[:, :, :, ::16] = a.astype(BF)
    w = np.array(f(rng, 128, 2048)).reshape(8, 16, 4, 8, 16, 4)
    w[:, 8:, :, :, :8] = 0
    for g in range(8):
        for h in range(8):
            if g != h: w[h, :, :, g, :8] = 0
    return {**d, **lists_of(rng), **weights(rng, w.reshape(128, 2048))}
def setup_inputs_near(rng):
    d = numbers_of(rng)
    m = np.stack([rng.permutation(8) + 1 for r in range(N)])
    s = rng.integers(0, 2 ** m[:, :, None], (N, 8, C + G))
    sg, o = signs(rng), rng.permutation(N)
    full = int(np.flatnonzero(o == 3)[0])
    h = 2 ** (m[full][:, None] - 1)
    s[full] = s[full] % h + h * ((np.arange(C + G) >= C // 2)[None, :] == (sg[full] > 0)[:, None])
    g = ((s[..., None] >> np.arange(8)) & 1) * np.exp2(np.arange(8) - 23.0)
    a = np.abs(np.concatenate([d["x"], d["gh"]], axis=2).astype(np.float32)).reshape(N, 8, 16, C + G, 4)
    a[:, :, 0] = 0
    a[:, :, 0, :, 0] = 0.5
    a[:, :, 8] = g[..., :4]
    a[:, :, 9] = g[..., 4:]
    a[:, :, 10:] = rng.integers(4, 8, (N, 8, 6, C + G, 4)) * 2.0 ** -20
    a = (a * np.float32(2.0 ** -7)).reshape(N, 128, 4 * (C + G)).astype(BF)
    k = sg * np.exp2(np.array([-30.0, 0.0, 24.0])[o % 3])[:, None]
    u = d["u"].reshape(N, 128, 128, 4)
    u[:, :, ::16] = 0
    for h in range(8):
        z = k[:, h].astype(np.float32).astype(BF)
        u[:, 16 * h, 16 * h, 0] = z
        u[:, 16 * h + 8:16 * h + 10, 16 * h] = z[:, None, None]
    return {**d, "x": np.ascontiguousarray(a[:, :, :4 * C]), "gh": np.ascontiguousarray(a[:, :, 4 * C:]), **lists_of(rng, (), (full,)), **still(rng)}
def setup_inputs_huge(rng):
    d = numbers_of(rng)
    a = 2.0 ** 29 * (0.6 + 0.4 * rng.random((N, 128, C + G, 4)))
    c = np.stack([rng.permutation(C + G) % 2 * 2.0 - 1.0 for r in range(N)])
    one = rng.permutation(N) < N // 2
    c[one] = 1
    a = (a * c[:, None, :, None]).astype(np.float32).reshape(N, 128, 4 * (C + G)).astype(BF)
    z = 2.0 ** 30 * (1 - 0.25 * rng.random((N, 128, 8, 4))) * signs(rng)[:, None, :, None]
    d["u"].reshape(N, 128, 128, 4)[:, :, ::16] = z.astype(np.float32).astype(BF)
    return {**d, "x": np.ascontiguousarray(a[:, :, :4 * C]), "gh": np.ascontiguousarray(a[:, :, 4 * C:]), **lists_of(rng, np.flatnonzero(~one)), **still(rng)}
def setup_inputs_shapes(rng):
    e = rng.permutation(N)
    kinds = np.stack([rng.permutation(8) for r in range(N)])
    kinds[e[0]] = 2
    kinds[e[1]] = 3
    nx = np.stack([linked(rng, kinds[r, g]) for r in range(N) for g in range(8)]).reshape(N, 8, C + G)
    j = np.arange(C)
    pr = np.zeros((N, 8, R, C), int)
    for r in range(N):
        o = rng.permutation(8)
        for g in range(8):
            for t in range(R): pr[r, g, t] = (j, j ^ 1, C - 1 - j, matching(rng, C // 2))[(o[g] + t) % 4]
    return {**numbers_of(rng), **stored(nx, pr), **weights(rng, f(rng, 128, 2048))}
def setup_inputs_spread(rng):
    d = setup_inputs(rng)
    d["x"] = big(wide(rng, N, 128, 4 * C, cols=6), 1)
    d["gh"] = big(wide(rng, N, 128, 4 * G, cols=6), 1)
    return d
def check_inputs(d):
    b = []
    for k in ("x", "gh", "u", "v"):
        a = np.abs(d[k].astype(np.float32))
        if not (np.isfinite(a).all() and ((a == 0) | (a >= 2.0 ** -30) & (a <= 2.0 ** 30)).all()): b.append("a value of " + k)
    for r in range(N):
        if (np.sort(gentries(d["nx"][r]), axis=1) != np.arange(C + G)).any(): b.append("nx of rank %d is no permutation in some group" % r)
        p = gentries(d["pr"][r]).reshape(8, R, C)
        if (p < 0).any() or (p >= C).any(): b.append("pr of rank %d out of range" % r)
        elif (np.take_along_axis(p, p, axis=2) != np.arange(C)).any(): b.append("pr of rank %d: a partner's partner is another column" % r)
    if (d["wc"] != d["wc"][:1]).any(): b.append("wc differs between ranks")
    s = [mx_ref.live(p) for p in d["ws"]]
    if any((p != s[0]).any() for p in s): b.append("ws differs between ranks")
    return b
def read(X, n):
    p = np.argsort(n, axis=1)
    return (gcols(X, n[:, :C]).astype(np.float32) + gcols(X, p[:, :C]).astype(np.float32)).astype(BF)
def reference(x, gh, u, v, nx, pr, wc, ws):
    w = pk(wc[0], ws[0])
    layer = [pick(w, np.arange(128 * b, 128 * b + 128)) for b in range(4)]
    qu = [mx_ref.quantize(u[r]) for r in range(N)]
    now = [np.concatenate([x[r], gh[r]], axis=1) for r in range(N)]
    link = [gentries(nx[r]) for r in range(N)]
    pair = [gentries(pr[r]).reshape(8, R, C) for r in range(N)]
    j = np.arange(C)
    for t in range(R):
        made = []
        for r in range(N):
            q = mx_ref.quantize(read(now[r], link[r]))
            s = mx_ref.matmul(qu[r], q)[::16] + np.float32(0.0)
            a, n = pair[r][:, t], link[r][:, :C]
            o = np.take_along_axis(s, a, axis=1)
            swap = (j < a) & (s < o) | (j > a) & (o < s)
            link[r] = np.concatenate([np.where(swap, np.take_along_axis(n, a, axis=1), n), link[r][:, C:]], axis=1)
            h = tile([np.maximum(mx_ref.matmul(layer[b], q), np.float32(0.0)) * np.float32(0.015625) for b in range(4)])
            made.append(decode(mx_ref.quantize(h)).astype(BF))
        for r in range(N):
            now[r] = np.concatenate([made[r], cut(made[r ^ (1 << t % L)], 0, 4 * G)], axis=1)
    y, nl = np.zeros((N, 128, C), np.float32), np.zeros((N, 8, C + G), np.float32)
    oc, osc = np.zeros((N, 128, 4 * C), np.uint8), np.zeros((N, 16, C), np.uint8)
    for r in range(N):
        q = mx_ref.quantize(read(now[r], link[r]))
        y[r] = mx_ref.matmul(mx_ref.quantize(v[r]), q)
        nl[r] = link[r]
        oc[r], osc[r] = emit(q)
    return {"y": y, "nl": nl, "oc": oc, "osc": osc}

@@ -1,0 +1,346 @@
+from concourse.mybir import dt, AluOpType, ActivationFunctionType
+
+C, G, R = 448, 256, 3
+W = C + G
+K = C // 16
+HALVES = (("A", 0, G), ("B", G, C))
+THIRDS = (("A", 0, G // 2), ("C", G // 2, G), ("B", G, C))
+WHOLE = (("", 0, C),)
+Q4, U8 = "float8_e4m3fn_x4", "uint8"
+STEP = 1024.0
+
+CFG = {"split": ("sc", "og", "gsig", "gpv", "scp"),
+       "ch": {0: THIRDS, 2: THIRDS, 3: (("A", 0, 320), ("B", 320, C))},
+       "lA": (0, 1, 2, 3), "lB": (2, 3, 6, 7), "lC": (6, 7, 0, 1), "ms": (4, 5),
+       "m": (2, 3, 6, 7), "mA": (2, 3, 6, 7), "mB": (0, 1, 4, 5), "mG": (0, 1, 4, 5)}
+
+SCRATCH = {
+    "nxi": ("sbuf", [128, W // 16], "int32"), "pri": ("sbuf", [128, R * K], "int32"),
+    "ut": ("sbuf", [128, 512], "bfloat16"), "vt": ("sbuf", [128, 512], "bfloat16"),
+    "uq": ("sbuf", [128, 128], Q4), "us": ("sbuf", [128, 128], U8),
+    "uq2": ("sbuf", [128, 128], Q4), "us2": ("sbuf", [128, 128], U8),
+    "vq": ("sbuf", [128, 128], Q4), "vs": ("sbuf", [128, 128], U8),
+    "wq": ("sbuf", [128, 512], Q4), "wsc": ("sbuf", [128, 512], U8),
+    "et": ("sbuf", [128, 2048], "bfloat16"), "ones": ("sbuf", [128, W], "bfloat16"),
+    "eq": ("sbuf", [128, 512], Q4), "es": ("sbuf", [128, 512], U8),
+    "pi": ("sbuf", [128, 8], "int32"), "ri": ("sbuf", [128, 8], "int32"), "uoi": ("sbuf", [128, 8], "int32"),
+    "uo": ("sbuf", [128, 8], "uint16"), "col": ("sbuf", [128, 8], "float32"),
+    "cnt": ("sbuf", [128, W], "float32"), "sig": ("sbuf", [128, W], "float32"),
+    "i16": ("sbuf", [128, C], "bfloat16"), "diag": ("sbuf", [128, C], "bfloat16"),
+    "c1": ("sbuf", [128, C], "bfloat16"), "c2": ("sbuf", [128, C], "float32"),
+    "j16": ("sbuf", [128, R * K], "float32"), "jf": ("sbuf", [128, R * K], "float32"),
+    "dj": ("sbuf", [128, R * K], "float32"), "r1": ("sbuf", [128, R * K], "float32"), "jb": ("sbuf", [128, R * K], "float32"),
+    "lh": ("sbuf", [128, 2 * R * K], "float32"), "lh16": ("sbuf", [128, 2 * R * K], "uint16"),
+    "nx16": ("sbuf", [128, W // 16], "uint16"),
+    "n4": ("sbuf", [128, 4 * K], "uint16"), "p4": ("sbuf", [128, 4 * K], "uint16"),
+    "pvf0": ("sbuf", [128, W], "float32"), "nxf0": ("sbuf", [128, W], "float32"),
+    "pvf": ("sbuf", [128, C], "float32"), "scn": ("sbuf", [128, C], "float32"), "scp": ("sbuf", [128, C], "float32"),
+    "sc": ("sbuf", [128, C], "float32"), "og": ("sbuf", [128, C], "float32"),
+    "sw": ("sbuf", [128, C], "bfloat16"), "t1": ("sbuf", [128, C], "bfloat16"),
+    "e1": ("sbuf", [128, K], "float32"), "e2": ("sbuf", [128, K], "float32"),
+    "so": ("sbuf", [128, K], "uint16"), "yt": ("sbuf", [128, C], "float32"),
+}
+for _t in range(R + 1):
+    SCRATCH["win%d" % _t] = ("sbuf", [128, 4 * W], "bfloat16")
+    SCRATCH["tmp%d" % _t] = ("sbuf", [128, 4 * C], "bfloat16")
+    SCRATCH["z%d" % _t] = ("sbuf", [128, 4 * C], "bfloat16")
+    SCRATCH["zq%d" % _t] = ("sbuf", [128, C], Q4)
+    SCRATCH["zs%d" % _t] = ("sbuf", [128, C], U8)
+    SCRATCH["po%d" % _t] = ("sbuf", [128, K], "uint16")
+for _t in range(R):
+    SCRATCH["h%d" % _t] = ("sbuf", [128, 4 * C], "bfloat16")
+    SCRATCH["hq%d" % _t] = ("sbuf", [128, C], Q4)
+    SCRATCH["hs%d" % _t] = ("sbuf", [128, C], U8)
+    SCRATCH["gq%d" % _t] = ("sbuf", [128, G], Q4)
+    SCRATCH["gs%d" % _t] = ("sbuf", [128, G], U8)
+    SCRATCH["nxf%d" % (_t + 1)] = ("sbuf", [128, C], "float32")
+    SCRATCH["no%d" % (_t + 1)] = ("sbuf", [128, K], "uint16")
+for _b in range(8):
+    SCRATCH["ps%d" % _b] = ("psum", [128, 512], "float32")
+
+LOADS = ["nx", "pr", "x", "gh", "u", "v", "wc", "ws"]
+SEMAPHORES = ["cV", "cS", "cP", "cG", "out", "sent"] + ["ld_" + n for n in LOADS] + ["arr%d" % t for t in range(R)]
+
+ORDER = {
+    "V": "ones cnt ri uo rf diag nx16 n43 scat n40 scan0 n42 n41 p43 p42 p40 p41 aA3.0 aA2.0 aA0.0 aA1.0 po0 zA.0 aB1.0 rA0.0 rA2.0 hA.0 aC1.0 aC3.0 aC0.0 aC2.0 qu zC.0 aB2.0 aB3.0 aB0.0 uq2 zB.0 hi lo hC.0 lh16 rB3.0 dj rB1.0 qe hB.0 ddB.0 ddA.0 t1.0 jb e1.0 e2.0 qv so.0 gsigA.0 gnx.0 scpB.0 scn.0 scpA.0 no.0 poA.0 dG3.0 gA2.1 poB.0 aA2.1 aA3.1 aA1.1 aA0.1 aB1.1 zA.1 aB0.1 aB3.1 aB2.1 zB.1 scA.1 hA.1 ogB.1 ddB.1 ddA.1 t1.1 e1.1 e2.1 so.1 hB.1 gsigA.1 d2.1 gpvA.1 scn.1 scpA.1 no.1 d0.1 dG0.1 scpB.1 poA.1 gA0.2 aA2.2 aA0.2 aA3.2 aA1.2 zA.2 aC0.2 aC3.2 rA0.2 rA3.2 poB.1 hA.2 aB1.2 aC1.2 aC2.2 aB3.2 zC.2 aB2.2 aB0.2 zB.2 hC.2 scB.2 ogB.2 ddB.2 ddA.2 t1.2 e1.2 e2.2 so.2 hB.2 gsigA.2 gpvB.2 gpvA.2 scpB.2 scpA.2 scn.2 poB.2 poA.2 no.2 dG0.2 dG3.2 gA3.3 aA0.3 aA3.3 aA1.3 aA2.3 zA.3 aB1.3 aB0.3 aB3.3 aB2.3 zB.3 yB",
+    "S": "ld_pr ld_gh et1 et0 b22 c2 b23 sigg b20 nxf et2 b21 gA3.0 gA2.0 gA0.0 gA1.0 gB1.0 gC1.0 gC2.0 rA1.0 rA3.0 gC3.0 gC0.0 c1 gB2.0 gB3.0 gB0.0 rC0.0 nb1 rC2.0 jf us2 rC3.0 rC1.0 scA.0 rB0.0 scB.0 rB2.0 ogB.0 ogA.0 r1 d0.0 d3.0 d1.0 gsigB.0 gpvB.0 gpvA.0 d2.0 dG2.0 dG1.0 gA3.1 dG0.0 gA1.1 gA0.1 gB1.1 gB0.1 gB3.1 gB2.1 rA0.1 rA2.1 rA3.1 rA1.1 scB.1 ogA.1 rB1.1 rB3.1 rB0.1 rB2.1 gsigB.1 gnx.1 d3.1 d1.1 gpvB.1 dG2.1 dG3.1 gA2.2 dG1.1 gA3.2 gA1.2 gC0.2 gC3.2 gB1.2 rA1.2 rA2.2 gC1.2 gC2.2 gB3.2 gB0.2 gB2.2 rC3.2 rC2.2 rC0.2 rC1.2 scA.2 ogA.2 rB0.2 rB2.2 rB1.2 rB3.2 gsigB.2 gnx.2 d2.2 d3.2 d0.2 d1.2 gA0.3 dG1.2 dG2.2 gA1.3 gA2.3 gB1.3 gB0.3 gB3.3 gB2.3 yA st_os0 st_os2 st_os1",
+    "P": "lA1.0 lA0.0 lA3.0 lA2.0 lC0.0 lC2.0 lC1.0 lC3.0 msA.0 lB3.0 lB0.0 msB.0 lB1.0 lB2.0 m0.0 m3.0 m1.0 m2.0 mG2.0 mG3.0 mG1.0 mG0.0 lA0.1 lA2.1 lA3.1 msA.1 lA1.1 msB.1 lB1.1 lB3.1 lB0.1 lB2.1 m2.1 m3.1 m0.1 m1.1 mG2.1 mG3.1 mG0.1 mG1.1 lA1.2 lA0.2 lA2.2 lA3.2 lC3.2 lC2.2 lC0.2 msA.2 lC1.2 msB.2 lB3.2 lB1.2 lB0.2 lB2.2 m1.2 m2.2 m0.2 m3.2 mG0.2 mG3.2 mG1.2 mG2.2 myA myB",
+    "G": "pi i16 uoi j16 E0 E1 E2 E3 sendq.0 sends.0 sendqC.0 sendsC.0 sendq.1 sends.1 sendq.2 sends.2 sendqC.2 sendsC.2",
+    "Y": "ld_nx ld_x ld_wc ld_ws ld_u ld_v st_nlg st_nlo st_ocA st_yA st_ocB st_os3 st_yB",
+}
+
+
+def plan():
+    return {q: ORDER[q].split() for q in ORDER}
+
+
+def meets(a, b):
+    if a[0] != b[0]:
+        return False
+    if a[0].startswith("ps"):
+        return True
+    if a[1] >= b[2] or b[1] >= a[2]:
+        return False
+    return not (a[3] == b[3] and (a[1] - b[1]) % a[3])
+
+
+def build(core, T, topo, where):
+    rank = T.rank_of(core)
+    A, F = AluOpType, ActivationFunctionType
+    ops = {}
+
+    def v(name, a=0, b=None, s=1):
+        return (name, a, SCRATCH[name][1][1] if b is None else b, s)
+
+    def ap(x):
+        return T[x[0]][:, x[1]:x[2]:x[3]] if x[3] > 1 else T[x[0]][:, x[1]:x[2]]
+
+    def op(name, on, call, reads, writes, sem=None, n=1):
+        ops[name] = (call, reads, writes, sem, n, on)
+
+    def bank(b, n):
+        return ("ps%d" % b, 0, n, 1)
+
+    def col(i):
+        return v("col", i, i + 1)
+
+    def views(*xs):
+        return [x for x in xs if isinstance(x, tuple)]
+
+    def arg(x):
+        return ap(x) if isinstance(x, tuple) else x
+
+    def ts(name, out, x, s1, o1, s2=None, o2=None):
+        if o2 is None:
+            op(name, "V", lambda q: q.tensor_scalar(ap(out), ap(x), arg(s1), None, o1), views(x, s1), [out])
+        else:
+            op(name, "V", lambda q: q.tensor_scalar(ap(out), ap(x), arg(s1), arg(s2), o1, o2), views(x, s1, s2), [out])
+
+    def tt(name, out, x, y, o, off=None):
+        op(name, "V", lambda q: q.tensor_tensor(ap(out), ap(x).indirect(ap(off)) if off else ap(x), ap(y), o), views(x, y, off), [out])
+
+    def act(name, out, x, f, scale=1.0, bias=0.0):
+        op(name, "S", lambda q: q.activation(ap(out), ap(x), f, bias=arg(bias), scale=arg(scale)), views(x, scale, bias), [out])
+
+    def move(name, out, x, off=None, relu=None, on="SV"):
+        def call(q):
+            src = ap(x).indirect(ap(off)) if off else ap(x)
+            if where[name] == "S":
+                return q.activation(ap(out), src, F.Relu, scale=relu) if relu else q.activation(ap(out), src, F.Copy)
+            return q.tensor_scalar(ap(out), src, 0.0, relu, A.max, A.mult) if relu else q.tensor_copy(ap(out), src)
+        op(name, on, call, views(x, off), [out])
+
+    def quant(name, qc, qs, x):
+        op(name, "V", lambda q: q.quantize_mx(ap(qc), ap(qs), ap(x)), [x], [qc, qs])
+
+    def mm(name, out, lc, ls, rc, rs):
+        op(name, "P", lambda q: q.matmul_mx(ap(out), ap(lc), ap(ls), ap(rc), ap(rs), True, True), [lc, ls, rc, rs], [out])
+
+    def scan(name, out, c, x):
+        op(name, "V", lambda q: q.tensor_tensor_scan(ap(out), ap(c), ap(x), 0.0, A.add, A.max), [c, x], [out])
+
+    def iota(name, out, pattern, base, mult, small=True):
+        if small:
+            op(name, "G", lambda q: q.iota(ap(out), pattern, base, mult, allow_small_or_imprecise_dtypes=True), [], [out])
+        else:
+            op(name, "G", lambda q: q.iota(ap(out), pattern, base, mult), [], [out])
+
+    def load(name, out, codes=False):
+        op("ld_" + name, "YS", lambda q: q.dma_start(ap(out).bitcast(dt.uint8) if codes else ap(out), T[name][:]), [], [out], "ld_" + name, 16)
+
+    def store(name, dst, src, x):
+        op(name, "YS", lambda q: q.dma_start(dst, src), [x], [], "out", 16)
+
+    def parts(name):
+        return HALVES if name in CFG["split"] else WHOLE
+
+    load("nx", v("nxi")); load("pr", v("pri")); load("x", v("win0", 0, 4 * C)); load("gh", v("win0", 4 * C))
+    load("wc", v("wq"), True); load("ws", v("wsc")); load("u", v("ut")); load("v", v("vt"))
+    iota("pi", v("pi"), [[0, 8]], 0, 1, False)
+    iota("i16", v("i16"), [[0, K], [1, 16]], 0, 0)
+    iota("j16", v("j16"), [[0, R], [16, K]], 0, 0)
+    iota("uoi", v("uoi"), [[16, 8]], 0, 0, False)
+    op("ones", "V", lambda q: q.memset(ap(v("ones")), 1.0), [], [v("ones")])
+    op("cnt", "V", lambda q: q.tensor_tensor_scan(ap(v("cnt")), ap(v("ones")), ap(v("ones")), -1.0, A.add, A.mult), [v("ones")], [v("cnt")])
+    for i, (a, e) in enumerate(((0, W), (W, 2 * W), (2 * W, 2048))):
+        act("et%d" % i, v("et", a, e), v("ones", 0, e - a), F.Copy, 0.0)
+    for b in range(4):
+        def unit(q, b=b):
+            return q.affine_select(ap(v("et", 512 * b + b, 512 * b + 512, 4)), ap(v("ones", 0, 128)), [[-1, 128]], A.is_equal, 0.0, 0, 1)
+        op("E%d" % b, "G", unit, [v("ones", 0, 128)], [v("et", 512 * b + b, 512 * b + 512, 4)])
+    ts("ri", v("ri"), v("pi"), 15, A.bitwise_and)
+    move("rf", col(0), v("ri", 0, 1), on="V")
+    ts("diag", v("diag"), v("i16"), col(0), A.is_equal)
+    act("c2", v("c2"), v("diag"), F.Identity, -33 * STEP, STEP)
+    act("c1", v("c1"), v("diag"), F.Identity, -33.0, 1.0)
+    for b in range(4):
+        act("b2%d" % b, col(4 + b), col(0), F.Identity, -STEP, 15 * STEP - b / 4)
+    move("nx16", v("nx16"), v("nxi"), on="V")
+    for b in range(4):
+        ts("n4%d" % b, v("n4", K * b, K * b + K), v("nxi", 0, K), 4.0, A.mult, float(b), A.add)
+    op("scat", "V", lambda q: q.tensor_copy(ap(v("pvf0")).indirect(ap(v("nx16"))), ap(v("cnt"))), [v("nx16"), v("cnt")], [v("pvf0")])
+    scan("scan0", v("scp"), v("c2"), v("pvf0", 0, C))
+    for b in range(4):
+        ts("p4%d" % b, v("p4", K * b, K * b + K), v("scp", 15, C, 16), col(4 + b), A.subtract, 4.0, A.mult)
+    ts("po0", v("po0"), v("scp", 15, C, 16), col(4), A.subtract)
+    act("nb1", col(2), col(0), F.Identity, 1.0, -15.0)
+    act("jf", v("jf"), v("j16"), F.Identity, 1.0, col(0))
+    tt("dj", v("dj"), v("pri"), v("jf"), A.subtract)
+    tt("lo", v("lh", 0, R * K), v("pri"), v("jf"), A.min)
+    tt("hi", v("lh", R * K), v("pri"), v("jf"), A.max)
+    move("lh16", v("lh16"), v("lh"), on="V")
+    act("r1", v("r1"), v("dj"), F.Identity, col(2))
+    tt("jb", v("jb"), v("r1"), v("jf"), A.add)
+    move("sigg", v("sig", C), v("cnt", C))
+    move("nxf", v("nxf0"), v("cnt"), v("nx16"))
+    store("st_nlg", T.nl[:, C:W], T.nxf0[0:128:16, C:W], v("nxf0", C))
+    move("uo", v("uo"), v("uoi"), on="V")
+    quant("qu", v("uq"), v("us"), v("ut"))
+    op("uq2", "V", lambda q: q.tensor_copy(T.uq2[:, 0:128].bitcast(dt.uint32), T.uq[:, 0:128].bitcast(dt.uint32).indirect(T.uo[:, 0:8])),
+       [v("uq"), v("uo")], [v("uq2")])
+    op("us2", "S", lambda q: q.activation(T.us2[:, 0:128], T.us[:, 0:128].indirect(T.uo[:, 0:8]), F.Copy), [v("us"), v("uo")], [v("us2")])
+    quant("qe", v("eq"), v("es"), v("et"))
+    quant("qv", v("vq"), v("vs"), v("vt"))
+
+    for t in range(R + 1):
+        win, z, zq, zs = "win%d" % t, "z%d" % t, "zq%d" % t, "zs%d" % t
+        ch = CFG["ch"].get(t, HALVES)
+        for c, a, e in ch:
+            for b in range(4):
+                if t == 0:
+                    w, o = v(win), K * b
+                    ln, lp = v("n4", o + a // 16, o + e // 16), v("p4", o + a // 16, o + e // 16)
+                else:
+                    w = v(win, W * b, W * b + W)
+                    ln, lp = v("no%d" % t, a // 16, e // 16), v("po%d" % t, a // 16, e // 16)
+                half = v("tmp%d" % t, C * b + a, C * b + e)
+                move("g%s%d.%d" % (c, b, t), half, w, ln)
+                tt("a%s%d.%d" % (c, b, t), v(z, 4 * a + b, 4 * e, 4), w, half, A.add, lp)
+            quant("z%s.%d" % (c, t), v(zq, a, e), v(zs, a, e), v(z, 4 * a, 4 * e))
+        if t == R:
+            break
+        h, hq, hs, gq, gs, nxt = "h%d" % t, "hq%d" % t, "hs%d" % t, "gq%d" % t, "gs%d" % t, "win%d" % (t + 1)
+        k = K * t
+
+        def layer(c, a, e):
+            for b in range(4):
+                s = bank(CFG["l" + c][b], e - a)
+                mm("l%s%d.%d" % (c, b, t), s, v("wq", 128 * b, 128 * b + 128), v("wsc", 128 * b, 128 * b + 128), v(zq, a, e), v(zs, a, e))
+                move("r%s%d.%d" % (c, b, t), v(h, 4 * a + b, 4 * e, 4), s, relu=0.015625)
+            quant("h%s.%d" % (c, t), v(hq, a, e), v(hs, a, e), v(h, 4 * a, 4 * e))
+        for x in ch[:-1]:
+            layer(*x)
+        peer = T.cores[rank ^ (1 << t % 2)]
+        assert topo.may_write(core, peer)
+        rid, pid, mask, ne = topo.addr(peer)[0], topo.addr(peer)[1], topo.mask(core, peer), len(topo.engines(core, peer))
+
+        def send(name, dst, src, codes, t=t, rid=rid, pid=pid, mask=mask, ne=ne):
+            def call(q):
+                o, i = (ap(dst).bitcast(dt.uint8), ap(src).bitcast(dt.uint8)) if codes else (ap(dst), ap(src))
+                q.remote_dma(o, i, T.sem["arr%d" % t], T.sem.sent, pid, rid, mask)
+            op(name, "G", call, [src], [], "sent", ne)
+        for c, a, e in ch[:-1]:
+            c = "" if c == "A" else c
+            send("sendq%s.%d" % (c, t), v(gq, a, e), v(hq, a, e), True)
+            send("sends%s.%d" % (c, t), v(gs, a, e), v(hs, a, e), False)
+        op("arr.%d" % t, "", None, [], [v(gq), v(gs)], "arr%d" % t, 2 * ne * (len(ch) - 1))
+        for i, (c, a, e) in enumerate(parts("sc")):
+            mm("ms%s.%d" % (c, t), bank(CFG["ms"][i], e - a), v("uq2"), v("us2"), v(zq, a, e), v(zs, a, e))
+            move("sc%s.%d" % (c, t), v("sc", a, e), bank(CFG["ms"][i], e - a))
+        for c, a, e in parts("og"):
+            move("og%s.%d" % (c, t), v("og", a, e), v("sc"), v("lh16", k + a // 16, k + e // 16))
+        for c, a, e in parts("og"):
+            tt("dd%s.%d" % (c, t), v("sw", a, e), v("sc"), v("og", a, e), A.is_gt, v("lh16", R * K + k + a // 16, R * K + k + e // 16))
+        scan("t1.%d" % t, v("t1"), v("c1"), v("sw"))
+        tt("e1.%d" % t, v("e1"), v("t1", 15, C, 16), v("dj", k, k + K), A.mult)
+        tt("e2.%d" % t, v("e2"), v("e1"), v("jb", k, k + K), A.add)
+        move("so.%d" % t, v("so"), v("e2"), on="V")
+        for c, a, e in parts("gsig"):
+            move("gsig%s.%d" % (c, t), v("sig", a, e), v("cnt", 0, C), v("so", a // 16, e // 16))
+        for c, a, e in parts("gnx"):
+            move("gnx%s.%d" % (c, t), v("nxf%d" % (t + 1), a, e), v("nxf%d" % t, 0, C), v("so", a // 16, e // 16))
+        for c, a, e in parts("gpv"):
+            move("gpv%s.%d" % (c, t), v("pvf", a, e), v("sig"), v("po%d" % t, a // 16, e // 16))
+        for c, a, e in parts("scn"):
+            scan("scn%s.%d" % (c, t), v("scn", a, e), v("c2", a, e), v("nxf%d" % (t + 1), a, e))
+            ts("no%s.%d" % (c, t), v("no%d" % (t + 1), a // 16, e // 16), v("scn", a + 15, e, 16), col(4), A.subtract)
+        for c, a, e in parts("scp"):
+            scan("scp%s.%d" % (c, t), v("scp", a, e), v("c2", a, e), v("pvf", a, e))
+            ts("po%s.%d" % (c, t), v("po%d" % (t + 1), a // 16, e // 16), v("scp", a + 15, e, 16), col(4), A.subtract)
+        layer(*ch[-1])
+        for c, qc, qs, a, e, o in [(c, hq, hs, a, e, a) for c, a, e in parts("m")] + [("G", gq, gs, 0, G, C)]:
+            for b in range(4):
+                s = bank(CFG["m" + c][b], e - a)
+                mm("m%s%d.%d" % (c, b, t), s, v("eq", 128 * b, 128 * b + 128), v("es", 128 * b, 128 * b + 128), v(qc, a, e), v(qs, a, e))
+                move("d%s%d.%d" % (c, b, t), v(nxt, W * b + o, W * b + o + e - a), s)
+    store("st_nlo", T.nl[:, 0:C], T["nxf%d" % R][0:128:16, :], v("nxf%d" % R))
+    for (c, a, e), b in zip(ch, (6, 7, 5)):
+        mm("my" + c, bank(b, e - a), v("vq"), v("vs"), v(zq, a, e), v(zs, a, e))
+        move("y" + c, v("yt", a, e), bank(b, e - a))
+        store("st_oc" + c, T.oc[:, 4 * a:4 * e], ap(v(zq, a, e)).bitcast(dt.uint8), v(zq, a, e))
+        store("st_y" + c, T.y[:, a:e], ap(v("yt", a, e)), v("yt", a, e))
+    for i in range(4):
+        store("st_os%d" % i, T.osc[4 * i:4 * i + 4, :], T[zs][32 * i:32 * i + 4, :], v(zs))
+    return ops
+
+
+def needs(ops):
+    names, need = list(ops), {}
+    for i, n in enumerate(names):
+        rd, wr = ops[n][1], ops[n][2]
+        need[n] = [m for m in names[:i]
+                   if any(meets(a, b) for a in ops[m][2] for b in rd + wr) or any(meets(a, b) for a in ops[m][1] for b in wr)
+                   or any(a[0].startswith("ps") and meets(a, b) for a in ops[m][1] for b in rd)]
+    return need
+
+
+def rank_program(g, core, T, topo):
+    if T.rank_of(core) is None:
+        return
+    order = plan()
+    where = {n: q for q in order for n in order[q]}
+    ops = build(core, T, topo, where)
+    assert sorted(n for n in ops if ops[n][0]) == sorted(where) and all(where[n] in ops[n][5] for n in where)
+    need = needs(ops)
+    mark, count = {}, {}
+    for q in order:
+        for n in order[q]:
+            s = ops[n][3] or "c" + q
+            count[s] = count.get(s, 0) + ops[n][4]
+            mark[n] = (s, count[s])
+    known = {q: {} for q in order}
+    after = {}
+    for t in range(R):
+        n = "arr.%d" % t
+        mark[n] = (ops[n][3], ops[n][4])
+        count[ops[n][3]] = ops[n][4]
+        after[n] = {ops[n][3]: ops[n][4]}
+    queues = {"V": g.vector, "S": g.scalar, "P": g.tensor, "G": g, "Y": g.sync}
+    at = {q: 0 for q in order}
+    while any(at[q] < len(order[q]) for q in order):
+        ready = [q for q in order if at[q] < len(order[q]) and all(m in after for m in need[order[q][at[q]]])]
+        assert ready, [order[q][at[q]] for q in order if at[q] < len(order[q])]
+        for q in ready:
+            n = order[q][at[q]]
+            at[q] += 1
+            want = {}
+            for m in need[n]:
+                s, c = mark[m]
+                if c > want.get(s, (0, None))[0]:
+                    want[s] = (c, m)
+            todo = [s for s in want if want[s][0] > known[q].get(s, 0)]
+            for s in todo:
+                if not any(o != s and after[want[o][1]].get(s, 0) >= want[s][0] for o in todo):
+                    queues[q].wait_ge(T.sem[s], want[s][0])
+            for s in todo:
+                for o, c in after[want[s][1]].items():
+                    known[q][o] = max(known[q].get(o, 0), c)
+            ins = ops[n][0](queues[q])
+            s, c = mark[n]
+            if ins is not None:
+                ins.then_inc(T.sem[s], ops[n][4])
+            after[n] = dict(known[q])
+            after[n][s] = c
+    for s in count:
+        if count[s] > max(known[q].get(s, 0) for q in order):
+            g.wait_ge(T.sem[s], count[s])

@@ -3,16 +3,24 @@ from concourse.mybir import dt, AluOpType, ActivationFunctionType
 C, G, R = 448, 256, 3
 W = C + G
 K = C // 16
-HALVES = (("A", 0, G), ("B", G, C))
-THIRDS = (("A", 0, G // 2), ("C", G // 2, G), ("B", G, C))
-WHOLE = (("", 0, C),)
 Q4, U8 = "float8_e4m3fn_x4", "uint8"
-STEP = 1024.0
+STEP, DROP = 1024.0, -4096.0
+LOW = 2.0 * W
 
-CFG = {"split": ("sc", "og", "gsig", "gpv", "scp"),
-       "ch": {0: THIRDS, 2: THIRDS, 3: (("A", 0, 320), ("B", 320, C))},
-       "lA": (0, 1, 2, 3), "lB": (2, 3, 6, 7), "lC": (6, 7, 0, 1), "ms": (4, 5),
-       "m": (2, 3, 6, 7), "mA": (2, 3, 6, 7), "mB": (0, 1, 4, 5), "mG": (0, 1, 4, 5)}
+
+def cuts(*at, end=C):
+    at = (0,) + at + (end,)
+    return tuple(("ABCDEFGH"[i], at[i], at[i + 1]) for i in range(len(at) - 1))
+
+
+CFG = {"g": {0: cuts(128, 256), 1: cuts(64, 128, 256, 352), 2: cuts(64, 128, 256, 352), 3: cuts(32, 64, 192, 320)},
+       "a": {0: cuts(128, 256), 1: cuts(128, 256, 352), 2: cuts(128, 256, 352), 3: cuts(64, 192, 320)},
+       "z": {0: cuts(128, 256), 1: cuts(128, 256), 2: cuts(128, 256), 3: cuts(320)},
+       "h": {t: cuts(256) for t in range(R)},
+       "send": {t: cuts(128, end=G) for t in range(R)},
+       "far": {t: 128 for t in range(R)},
+       "split": {"og": cuts(256), "sc": cuts(256), "gsig": cuts(256), "s0": cuts(128), "m": cuts(256)},
+       "l": ((0, 1, 2, 3), (6, 7, 0, 1), (2, 3, 6, 7)), "lG": (2, 3, 6, 7), "ms": (4, 5), "m": (0, 1, 4, 5), "mG": (2, 3, 6, 7)}
 
 SCRATCH = {
     "nxi": ("sbuf", [128, W // 16], "int32"), "pri": ("sbuf", [128, R * K], "int32"),
@@ -21,23 +29,23 @@ SCRATCH = {
     "uq2": ("sbuf", [128, 128], Q4), "us2": ("sbuf", [128, 128], U8),
     "vq": ("sbuf", [128, 128], Q4), "vs": ("sbuf", [128, 128], U8),
     "wq": ("sbuf", [128, 512], Q4), "wsc": ("sbuf", [128, 512], U8),
-    "et": ("sbuf", [128, 2048], "bfloat16"), "ones": ("sbuf", [128, W], "bfloat16"),
+    "et": ("sbuf", [128, 516], "bfloat16"), "ones": ("sbuf", [128, W], "bfloat16"),
     "eq": ("sbuf", [128, 512], Q4), "es": ("sbuf", [128, 512], U8),
-    "pi": ("sbuf", [128, 8], "int32"), "ri": ("sbuf", [128, 8], "int32"), "uoi": ("sbuf", [128, 8], "int32"),
-    "uo": ("sbuf", [128, 8], "uint16"), "col": ("sbuf", [128, 8], "float32"),
+    "pi": ("sbuf", [128, K], "int32"), "p16": ("sbuf", [128, K], "uint16"), "ri": ("sbuf", [128, 4], "int32"),
+    "uoi": ("sbuf", [128, 8], "int32"), "uo": ("sbuf", [128, 8], "uint16"), "col": ("sbuf", [128, 8], "float32"),
     "cnt": ("sbuf", [128, W], "float32"), "sig": ("sbuf", [128, W], "float32"),
-    "i16": ("sbuf", [128, C], "bfloat16"), "diag": ("sbuf", [128, C], "bfloat16"),
-    "c1": ("sbuf", [128, C], "bfloat16"), "c2": ("sbuf", [128, C], "float32"),
-    "j16": ("sbuf", [128, R * K], "float32"), "jf": ("sbuf", [128, R * K], "float32"),
-    "dj": ("sbuf", [128, R * K], "float32"), "r1": ("sbuf", [128, R * K], "float32"), "jb": ("sbuf", [128, R * K], "float32"),
+    "f16": ("sbuf", [128, 128], "bfloat16"), "f4": ("sbuf", [128, 128], "bfloat16"),
+    "c16": ("sbuf", [128, C], "bfloat16"), "c4": ("sbuf", [128, C], "bfloat16"),
+    "j16": ("sbuf", [128, R * K], "float32"), "jf": ("sbuf", [128, R * K], "float32"), "dj": ("sbuf", [128, R * K], "float32"),
+    "kd": ("sbuf", [128, R * K], "float32"), "jb": ("sbuf", [128, R * K], "float32"),
     "lh": ("sbuf", [128, 2 * R * K], "float32"), "lh16": ("sbuf", [128, 2 * R * K], "uint16"),
-    "nx16": ("sbuf", [128, W // 16], "uint16"),
-    "n4": ("sbuf", [128, 4 * K], "uint16"), "p4": ("sbuf", [128, 4 * K], "uint16"),
-    "pvf0": ("sbuf", [128, W], "float32"), "nxf0": ("sbuf", [128, W], "float32"),
-    "pvf": ("sbuf", [128, C], "float32"), "scn": ("sbuf", [128, C], "float32"), "scp": ("sbuf", [128, C], "float32"),
-    "sc": ("sbuf", [128, C], "float32"), "og": ("sbuf", [128, C], "float32"),
-    "sw": ("sbuf", [128, C], "bfloat16"), "t1": ("sbuf", [128, C], "bfloat16"),
     "e1": ("sbuf", [128, K], "float32"), "e2": ("sbuf", [128, K], "float32"),
+    "nx16": ("sbuf", [128, W // 16], "uint16"), "n4": ("sbuf", [128, 4 * K], "uint16"),
+    "pvf0": ("sbuf", [128, W], "float32"), "nxf0": ("sbuf", [128, W], "float32"),
+    "scn": ("sbuf", [128, C], "float32"), "s0": ("sbuf", [128, C], "float32"),
+    "pvh": ("sbuf", [128, C], "float16"), "s4": ("sbuf", [128, C], "float16"), "s16": ("sbuf", [128, C], "float16"),
+    "sc": ("sbuf", [128, C], "float32"), "og": ("sbuf", [128, C], "float32"),
+    "sw": ("sbuf", [128, C], "bfloat16"), "t1": ("sbuf", [128, C], "float16"),
     "so": ("sbuf", [128, K], "uint16"), "yt": ("sbuf", [128, C], "float32"),
 }
 for _t in range(R + 1):
@@ -46,28 +54,26 @@ for _t in range(R + 1):
     SCRATCH["z%d" % _t] = ("sbuf", [128, 4 * C], "bfloat16")
     SCRATCH["zq%d" % _t] = ("sbuf", [128, C], Q4)
     SCRATCH["zs%d" % _t] = ("sbuf", [128, C], U8)
-    SCRATCH["po%d" % _t] = ("sbuf", [128, K], "uint16")
+    SCRATCH["pq%d" % _t] = ("sbuf", [128, 4 * K], "uint16")
 for _t in range(R):
+    SCRATCH["po%d" % _t] = ("sbuf", [128, K], "uint16")
     SCRATCH["h%d" % _t] = ("sbuf", [128, 4 * C], "bfloat16")
     SCRATCH["hq%d" % _t] = ("sbuf", [128, C], Q4)
     SCRATCH["hs%d" % _t] = ("sbuf", [128, C], U8)
     SCRATCH["gq%d" % _t] = ("sbuf", [128, G], Q4)
     SCRATCH["gs%d" % _t] = ("sbuf", [128, G], U8)
+    SCRATCH["fq%d" % _t] = ("sbuf", [128, G], Q4)
+    SCRATCH["fs%d" % _t] = ("sbuf", [128, G], U8)
+    SCRATCH["fh%d" % _t] = ("sbuf", [128, 4 * G], "bfloat16")
     SCRATCH["nxf%d" % (_t + 1)] = ("sbuf", [128, C], "float32")
-    SCRATCH["no%d" % (_t + 1)] = ("sbuf", [128, K], "uint16")
+    SCRATCH["nq%d" % (_t + 1)] = ("sbuf", [128, 4 * K], "uint16")
 for _b in range(8):
     SCRATCH["ps%d" % _b] = ("psum", [128, 512], "float32")
 
 LOADS = ["nx", "pr", "x", "gh", "u", "v", "wc", "ws"]
-SEMAPHORES = ["cV", "cS", "cP", "cG", "out", "sent"] + ["ld_" + n for n in LOADS] + ["arr%d" % t for t in range(R)]
+SEMAPHORES = ["cV", "cS", "cP", "cG", "out", "sent"] + ["ld_" + n for n in LOADS] + ["arr%s%d" % (c, t) for t in range(R) for c in "FH"]
 
-ORDER = {
-    "V": "ones cnt ri uo rf diag nx16 n43 scat n40 scan0 n42 n41 p43 p42 p40 p41 aA3.0 aA2.0 aA0.0 aA1.0 po0 zA.0 aB1.0 rA0.0 rA2.0 hA.0 aC1.0 aC3.0 aC0.0 aC2.0 qu zC.0 aB2.0 aB3.0 aB0.0 uq2 zB.0 hi lo hC.0 lh16 rB3.0 dj rB1.0 qe hB.0 ddB.0 ddA.0 t1.0 jb e1.0 e2.0 qv so.0 gsigA.0 gnx.0 scpB.0 scn.0 scpA.0 no.0 poA.0 dG3.0 gA2.1 poB.0 aA2.1 aA3.1 aA1.1 aA0.1 aB1.1 zA.1 aB0.1 aB3.1 aB2.1 zB.1 scA.1 hA.1 ogB.1 ddB.1 ddA.1 t1.1 e1.1 e2.1 so.1 hB.1 gsigA.1 d2.1 gpvA.1 scn.1 scpA.1 no.1 d0.1 dG0.1 scpB.1 poA.1 gA0.2 aA2.2 aA0.2 aA3.2 aA1.2 zA.2 aC0.2 aC3.2 rA0.2 rA3.2 poB.1 hA.2 aB1.2 aC1.2 aC2.2 aB3.2 zC.2 aB2.2 aB0.2 zB.2 hC.2 scB.2 ogB.2 ddB.2 ddA.2 t1.2 e1.2 e2.2 so.2 hB.2 gsigA.2 gpvB.2 gpvA.2 scpB.2 scpA.2 scn.2 poB.2 poA.2 no.2 dG0.2 dG3.2 gA3.3 aA0.3 aA3.3 aA1.3 aA2.3 zA.3 aB1.3 aB0.3 aB3.3 aB2.3 zB.3 yB",
-    "S": "ld_pr ld_gh et1 et0 b22 c2 b23 sigg b20 nxf et2 b21 gA3.0 gA2.0 gA0.0 gA1.0 gB1.0 gC1.0 gC2.0 rA1.0 rA3.0 gC3.0 gC0.0 c1 gB2.0 gB3.0 gB0.0 rC0.0 nb1 rC2.0 jf us2 rC3.0 rC1.0 scA.0 rB0.0 scB.0 rB2.0 ogB.0 ogA.0 r1 d0.0 d3.0 d1.0 gsigB.0 gpvB.0 gpvA.0 d2.0 dG2.0 dG1.0 gA3.1 dG0.0 gA1.1 gA0.1 gB1.1 gB0.1 gB3.1 gB2.1 rA0.1 rA2.1 rA3.1 rA1.1 scB.1 ogA.1 rB1.1 rB3.1 rB0.1 rB2.1 gsigB.1 gnx.1 d3.1 d1.1 gpvB.1 dG2.1 dG3.1 gA2.2 dG1.1 gA3.2 gA1.2 gC0.2 gC3.2 gB1.2 rA1.2 rA2.2 gC1.2 gC2.2 gB3.2 gB0.2 gB2.2 rC3.2 rC2.2 rC0.2 rC1.2 scA.2 ogA.2 rB0.2 rB2.2 rB1.2 rB3.2 gsigB.2 gnx.2 d2.2 d3.2 d0.2 d1.2 gA0.3 dG1.2 dG2.2 gA1.3 gA2.3 gB1.3 gB0.3 gB3.3 gB2.3 yA st_os0 st_os2 st_os1",
-    "P": "lA1.0 lA0.0 lA3.0 lA2.0 lC0.0 lC2.0 lC1.0 lC3.0 msA.0 lB3.0 lB0.0 msB.0 lB1.0 lB2.0 m0.0 m3.0 m1.0 m2.0 mG2.0 mG3.0 mG1.0 mG0.0 lA0.1 lA2.1 lA3.1 msA.1 lA1.1 msB.1 lB1.1 lB3.1 lB0.1 lB2.1 m2.1 m3.1 m0.1 m1.1 mG2.1 mG3.1 mG0.1 mG1.1 lA1.2 lA0.2 lA2.2 lA3.2 lC3.2 lC2.2 lC0.2 msA.2 lC1.2 msB.2 lB3.2 lB1.2 lB0.2 lB2.2 m1.2 m2.2 m0.2 m3.2 mG0.2 mG3.2 mG1.2 mG2.2 myA myB",
-    "G": "pi i16 uoi j16 E0 E1 E2 E3 sendq.0 sends.0 sendqC.0 sendsC.0 sendq.1 sends.1 sendq.2 sends.2 sendqC.2 sendsC.2",
-    "Y": "ld_nx ld_x ld_wc ld_ws ld_u ld_v st_nlg st_nlo st_ocA st_yA st_ocB st_os3 st_yB",
-}
+ORDER = {'V': 'f4a ones r2 r0 r1 f16a p16 rf cnt uo k6 nx16 n41 n40 n42 scat n43 s0A gA3.0 pq0A s0B aA.0 pq0B zA.0 aB.0 zB.0 qu dj uq2 aC.0 zC.0 lo qe2 hi qe3 lh16 hA.0 qe0 s1 qe1 ddA.0 ddB.0 rB0.0 t1.0 rB3.0 e1.0 jb hB.0 e2.0 qv so.0 po0 rF0.0 rF3.0 gsigB.0 hF.0 dB2.0 gpv.0 scn.0 s4.0 nq.0 dG1.0 dG2.0 pq.0 gB.1 aA.1 aB.1 zA.1 zB.1 aC.1 aD.1 zC.1 s16.0 scB.1 hA.1 ogB.1 po.0 ddB.1 ddA.1 dA0.1 t1.1 hB.1 e1.1 dA1.1 e2.1 rF2.1 so.1 rF1.1 gsigA.1 hF.1 dB0.1 gpv.1 scn.1 dB2.1 dG0.1 s4.1 nq.1 pq.1 gB.2 aA.2 aB.2 zA.2 zB.2 aD.2 aC.2 zC.2 rA1.2 s16.1 hA.2 ogB.2 rB1.2 ddB.2 ddA.2 rB2.2 t1.2 po.1 e1.2 hB.2 e2.2 rF3.2 so.2 rF0.2 dA2.2 hF.2 dB2.2 dB0.2 gpv.2 scn.2 s4.2 dG2.2 dG1.2 nq.2 pq.2 gB.3 gA.3 aA.3 aB.3 aC.3 zA.3 aD.3 zB.3 yB', 'S': 'ld_gh k3 c4 k4 nxf k5 jf c16 k7 gA0.0 gA1.0 gA2.0 gB2.0 gB0.0 gB3.0 gB1.0 gC2.0 gC3.0 gC0.0 gC1.0 us2 kd rA3.0 rA0.0 rA2.0 scA.0 rA1.0 scB.0 rB2.0 ogA.0 ogB.0 dA3.0 dA2.0 rB1.0 dA0.0 dA1.0 rF1.0 rF2.0 gsigA.0 gnx.0 dB0.0 dB1.0 dB3.0 dG0.0 dG3.0 gA.1 gC.1 gD.1 gE.1 rA0.1 rA2.1 rA1.1 rA3.1 scA.1 rB3.1 ogA.1 rB1.1 rB0.1 rB2.1 dA2.1 dA3.1 rF0.1 rF3.1 gsigB.1 gnx.1 dB3.1 dB1.1 dG1.1 dG3.1 dG2.1 gA.2 gC.2 gE.2 gD.2 rA3.2 rA2.2 rA0.2 scA.2 scB.2 rB3.2 ogA.2 rB0.2 dA3.2 dA0.2 dA1.2 rF1.2 rF2.2 gsigA.2 gsigB.2 gnx.2 dB1.2 dB3.2 dG0.2 dG3.2 gC.3 gD.3 gE.3 yA st_os0 st_os1', 'P': 'lA0.0 lA3.0 lA2.0 msA.0 lA1.0 msB.0 lB2.0 lB0.0 lB3.0 mA3.0 mA2.0 lB1.0 mA1.0 mA0.0 lF1.0 lF0.0 lF2.0 lF3.0 mB1.0 mB0.0 mB2.0 mB3.0 mG0.0 mG1.0 mG3.0 mG2.0 lA0.1 lA2.1 lA1.1 lA3.1 msA.1 msB.1 lB3.1 lB0.1 lB1.1 mA0.1 lB2.1 mA2.1 mA1.1 mA3.1 lF2.1 lF0.1 lF3.1 lF1.1 mB2.1 mB0.1 mB3.1 mB1.1 mG1.1 mG3.1 mG0.1 mG2.1 lA3.2 lA2.2 lA0.2 lA1.2 msA.2 msB.2 lB3.2 lB0.2 lB1.2 mA0.2 mA3.2 mA1.2 lB2.2 lF1.2 lF3.2 lF2.2 lF0.2 mA2.2 mB2.2 mB0.2 mB3.2 mB1.2 mG0.2 mG2.2 mG3.2 mG1.2 myA myB', 'G': 'pi f4b f4c uoi j16 f16b f16c E sigg sendFqA.0 sendFsA.0 sendHqB.0 sendHsB.0 sendFqA.1 sendFsA.1 sendHqB.1 sendHsB.1 sendFqA.2 sendFsA.2 sendHqB.2 sendHsB.2', 'Y': 'ld_nx ld_x ld_pr ld_wc ld_ws ld_u ld_v st_nlg st_nlo st_ocA st_yA st_ocB st_os2 st_os3 st_yB'}
 
 
 def plan():
@@ -110,9 +116,9 @@ def build(core, T, topo, where):
     def arg(x):
         return ap(x) if isinstance(x, tuple) else x
 
-    def ts(name, out, x, s1, o1, s2=None, o2=None):
+    def ts(name, out, x, s1, o1, s2=None, o2=None, off=None):
         if o2 is None:
-            op(name, "V", lambda q: q.tensor_scalar(ap(out), ap(x), arg(s1), None, o1), views(x, s1), [out])
+            op(name, "V", lambda q: q.tensor_scalar(ap(out), ap(x).indirect(ap(off)) if off else ap(x), arg(s1), None, o1), views(x, s1, off), [out])
         else:
             op(name, "V", lambda q: q.tensor_scalar(ap(out), ap(x), arg(s1), arg(s2), o1, o2), views(x, s1, s2), [out])
 
@@ -130,14 +136,17 @@ def build(core, T, topo, where):
             return q.tensor_scalar(ap(out), src, 0.0, relu, A.max, A.mult) if relu else q.tensor_copy(ap(out), src)
         op(name, on, call, views(x, off), [out])
 
+    def fill(name, out, c):
+        op(name, "V", lambda q: q.memset(ap(out), c), [], [out])
+
     def quant(name, qc, qs, x):
         op(name, "V", lambda q: q.quantize_mx(ap(qc), ap(qs), ap(x)), [x], [qc, qs])
 
     def mm(name, out, lc, ls, rc, rs):
         op(name, "P", lambda q: q.matmul_mx(ap(out), ap(lc), ap(ls), ap(rc), ap(rs), True, True), [lc, ls, rc, rs], [out])
 
-    def scan(name, out, c, x):
-        op(name, "V", lambda q: q.tensor_tensor_scan(ap(out), ap(c), ap(x), 0.0, A.add, A.max), [c, x], [out])
+    def scan(name, out, c, x, first=0.0, o0=A.add, o1=A.max):
+        op(name, "V", lambda q: q.tensor_tensor_scan(ap(out), ap(c), ap(x), first, o0, o1), [c, x], [out])
 
     def iota(name, out, pattern, base, mult, small=True):
         if small:
@@ -145,53 +154,63 @@ def build(core, T, topo, where):
         else:
             op(name, "G", lambda q: q.iota(ap(out), pattern, base, mult), [], [out])
 
-    def load(name, out, codes=False):
-        op("ld_" + name, "YS", lambda q: q.dma_start(ap(out).bitcast(dt.uint8) if codes else ap(out), T[name][:]), [], [out], "ld_" + name, 16)
+    def select(name, out, x, pattern, o, other, base, mult):
+        op(name, "G", lambda q: q.affine_select(ap(out), ap(x), pattern, o, other, base, mult), [x], [out])
+
+    def load(name, out, codes=False, after=None):
+        op("ld_" + name, "YS", lambda q: q.dma_start(ap(out).bitcast(dt.uint8) if codes else ap(out), T[name][:]), views(after), [out], "ld_" + name, 16)
 
     def store(name, dst, src, x):
         op(name, "YS", lambda q: q.dma_start(dst, src), [x], [], "out", 16)
 
     def parts(name):
-        return HALVES if name in CFG["split"] else WHOLE
+        return CFG["split"].get(name, (("", 0, C),))
 
     load("nx", v("nxi")); load("pr", v("pri")); load("x", v("win0", 0, 4 * C)); load("gh", v("win0", 4 * C))
-    load("wc", v("wq"), True); load("ws", v("wsc")); load("u", v("ut")); load("v", v("vt"))
-    iota("pi", v("pi"), [[0, 8]], 0, 1, False)
-    iota("i16", v("i16"), [[0, K], [1, 16]], 0, 0)
+    load("wc", v("wq"), True, v("nxi")); load("ws", v("wsc")); load("u", v("ut")); load("v", v("vt"))
+    iota("pi", v("pi"), [[0, K]], 0, 1, False)
     iota("j16", v("j16"), [[0, R], [16, K]], 0, 0)
     iota("uoi", v("uoi"), [[16, 8]], 0, 0, False)
-    op("ones", "V", lambda q: q.memset(ap(v("ones")), 1.0), [], [v("ones")])
-    op("cnt", "V", lambda q: q.tensor_tensor_scan(ap(v("cnt")), ap(v("ones")), ap(v("ones")), -1.0, A.add, A.mult), [v("ones")], [v("cnt")])
-    for i, (a, e) in enumerate(((0, W), (W, 2 * W), (2 * W, 2048))):
-        act("et%d" % i, v("et", a, e), v("ones", 0, e - a), F.Copy, 0.0)
+    fill("ones", v("ones"), 1.0)
+    scan("cnt", v("cnt"), v("ones"), v("ones"), -1.0, A.add, A.mult)
+    select("E", v("et"), v("ones", 0, 516), [[1, 516]], A.is_equal, 0.0, -3, -4)
     for b in range(4):
-        def unit(q, b=b):
-            return q.affine_select(ap(v("et", 512 * b + b, 512 * b + 512, 4)), ap(v("ones", 0, 128)), [[-1, 128]], A.is_equal, 0.0, 0, 1)
-        op("E%d" % b, "G", unit, [v("ones", 0, 128)], [v("et", 512 * b + b, 512 * b + 512, 4)])
-    ts("ri", v("ri"), v("pi"), 15, A.bitwise_and)
-    move("rf", col(0), v("ri", 0, 1), on="V")
-    ts("diag", v("diag"), v("i16"), col(0), A.is_equal)
-    act("c2", v("c2"), v("diag"), F.Identity, -33 * STEP, STEP)
-    act("c1", v("c1"), v("diag"), F.Identity, -33.0, 1.0)
-    for b in range(4):
-        act("b2%d" % b, col(4 + b), col(0), F.Identity, -STEP, 15 * STEP - b / 4)
+        quant("qe%d" % b, v("eq", 128 * b, 128 * b + 128), v("es", 128 * b, 128 * b + 128), v("et", 3 - b, 515 - b))
+    move("p16", v("p16"), v("pi"), on="V")
+    fill("f4a", v("f4"), DROP)
+    select("f4b", v("f4"), v("f4"), [[-16, 8], [0, 4], [-4, 4]], A.is_ge, float(W), 0, 1)
+    select("f4c", v("f4"), v("f4"), [[16, 8], [0, 4], [4, 4]], A.is_ge, float(W), 3, -1)
+    move("c4", v("c4"), v("f4"), v("p16"))
+    fill("f16a", v("f16"), 0.0)
+    select("f16b", v("f16"), v("f16"), [[1, 128]], A.not_equal, DROP, 0, -1)
+    select("f16c", v("f16"), v("f16"), [[1, 128]], A.not_equal, STEP, -1, -1)
+    move("c16", v("c16"), v("f16"), v("p16"))
+    ts("r0", v("ri", 0, 1), v("pi", 0, 1), 15, A.bitwise_and)
+    ts("r1", v("ri", 1, 2), v("pi", 0, 1), 2, A.logical_shift_right, 3, A.bitwise_and)
+    ts("r2", v("ri", 2, 3), v("pi", 0, 1), 3, A.bitwise_and)
+    move("rf", v("col", 0, 3), v("ri", 0, 3), on="V")
+    act("k3", col(7), col(1), F.Identity, 4.0 * W, -12.0 * W)
+    act("k4", col(3), col(7), F.Identity, 1.0, col(2))
+    act("k5", col(4), col(3), F.Identity, 1.0, 4 * LOW)
+    ts("k6", col(5), col(0), 15.0, A.is_lt, STEP, A.mult)
+    act("k7", col(6), col(5), F.Copy, -1.0)
     move("nx16", v("nx16"), v("nxi"), on="V")
     for b in range(4):
         ts("n4%d" % b, v("n4", K * b, K * b + K), v("nxi", 0, K), 4.0, A.mult, float(b), A.add)
     op("scat", "V", lambda q: q.tensor_copy(ap(v("pvf0")).indirect(ap(v("nx16"))), ap(v("cnt"))), [v("nx16"), v("cnt")], [v("pvf0")])
-    scan("scan0", v("scp"), v("c2"), v("pvf0", 0, C))
-    for b in range(4):
-        ts("p4%d" % b, v("p4", K * b, K * b + K), v("scp", 15, C, 16), col(4 + b), A.subtract, 4.0, A.mult)
-    ts("po0", v("po0"), v("scp", 15, C, 16), col(4), A.subtract)
-    act("nb1", col(2), col(0), F.Identity, 1.0, -15.0)
+    for c, a, e in parts("s0"):
+        scan("s0" + c, v("scn", a, e), v("c4", a, e), v("pvf0", a, e))
+        ts("pq0" + c, v("pq0", a // 4, e // 4), v("scn", a + 3, e, 4), 4.0, A.mult, col(3), A.add)
+    scan("s1", v("s0"), v("c16"), v("pvf0", 0, C))
+    ts("po0", v("po0"), v("s0", 15, C, 16), col(5), A.subtract)
     act("jf", v("jf"), v("j16"), F.Identity, 1.0, col(0))
     tt("dj", v("dj"), v("pri"), v("jf"), A.subtract)
     tt("lo", v("lh", 0, R * K), v("pri"), v("jf"), A.min)
     tt("hi", v("lh", R * K), v("pri"), v("jf"), A.max)
     move("lh16", v("lh16"), v("lh"), on="V")
-    act("r1", v("r1"), v("dj"), F.Identity, col(2))
-    tt("jb", v("jb"), v("r1"), v("jf"), A.add)
-    move("sigg", v("sig", C), v("cnt", C))
+    act("kd", v("kd"), v("dj"), F.Identity, col(6))
+    tt("jb", v("jb"), v("kd"), v("jf"), A.add)
+    iota("sigg", v("sig", C), [[1, G]], C, 0)
     move("nxf", v("nxf0"), v("cnt"), v("nx16"))
     store("st_nlg", T.nl[:, C:W], T.nxf0[0:128:16, C:W], v("nxf0", C))
     move("uo", v("uo"), v("uoi"), on="V")
@@ -199,80 +218,90 @@ def build(core, T, topo, where):
     op("uq2", "V", lambda q: q.tensor_copy(T.uq2[:, 0:128].bitcast(dt.uint32), T.uq[:, 0:128].bitcast(dt.uint32).indirect(T.uo[:, 0:8])),
        [v("uq"), v("uo")], [v("uq2")])
     op("us2", "S", lambda q: q.activation(T.us2[:, 0:128], T.us[:, 0:128].indirect(T.uo[:, 0:8]), F.Copy), [v("us"), v("uo")], [v("us2")])
-    quant("qe", v("eq"), v("es"), v("et"))
     quant("qv", v("vq"), v("vs"), v("vt"))
 
     for t in range(R + 1):
-        win, z, zq, zs = "win%d" % t, "z%d" % t, "zq%d" % t, "zs%d" % t
-        ch = CFG["ch"].get(t, HALVES)
+        win, tmp, z, zq, zs = "win%d" % t, "tmp%d" % t, "z%d" % t, "zq%d" % t, "zs%d" % t
+        for c, a, e in CFG["g"][t]:
+            if t == 0:
+                for b in range(4):
+                    move("g%s%d.0" % (c, b), v(tmp, 4 * a + b, 4 * e, 4), v(win), v("n4", K * b + a // 16, K * b + e // 16))
+            else:
+                move("g%s.%d" % (c, t), v(tmp, 4 * a, 4 * e), v(win), v("nq%d" % t, a // 4, e // 4))
+        for c, a, e in CFG["a"][t]:
+            tt("a%s.%d" % (c, t), v(z, 4 * a, 4 * e), v(win), v(tmp, 4 * a, 4 * e), A.add, v("pq%d" % t, a // 4, e // 4))
+        ch = CFG["z"][t]
         for c, a, e in ch:
-            for b in range(4):
-                if t == 0:
-                    w, o = v(win), K * b
-                    ln, lp = v("n4", o + a // 16, o + e // 16), v("p4", o + a // 16, o + e // 16)
-                else:
-                    w = v(win, W * b, W * b + W)
-                    ln, lp = v("no%d" % t, a // 16, e // 16), v("po%d" % t, a // 16, e // 16)
-                half = v("tmp%d" % t, C * b + a, C * b + e)
-                move("g%s%d.%d" % (c, b, t), half, w, ln)
-                tt("a%s%d.%d" % (c, b, t), v(z, 4 * a + b, 4 * e, 4), w, half, A.add, lp)
             quant("z%s.%d" % (c, t), v(zq, a, e), v(zs, a, e), v(z, 4 * a, 4 * e))
         if t == R:
             break
         h, hq, hs, gq, gs, nxt = "h%d" % t, "hq%d" % t, "hs%d" % t, "gq%d" % t, "gs%d" % t, "win%d" % (t + 1)
+        fq, fs, fh, far = "fq%d" % t, "fs%d" % t, "fh%d" % t, CFG["far"][t]
         k = K * t
 
-        def layer(c, a, e):
+        def layer(banks, c, a, e, zq=zq, zs=zs, h=h, hq=hq, hs=hs):
             for b in range(4):
-                s = bank(CFG["l" + c][b], e - a)
+                s = bank(banks[b], e - a)
                 mm("l%s%d.%d" % (c, b, t), s, v("wq", 128 * b, 128 * b + 128), v("wsc", 128 * b, 128 * b + 128), v(zq, a, e), v(zs, a, e))
                 move("r%s%d.%d" % (c, b, t), v(h, 4 * a + b, 4 * e, 4), s, relu=0.015625)
             quant("h%s.%d" % (c, t), v(hq, a, e), v(hs, a, e), v(h, 4 * a, 4 * e))
-        for x in ch[:-1]:
-            layer(*x)
+        for i, x in enumerate(CFG["h"][t][:-1]):
+            layer(CFG["l"][i], *x)
         peer = T.cores[rank ^ (1 << t % 2)]
         assert topo.may_write(core, peer)
         rid, pid, mask, ne = topo.addr(peer)[0], topo.addr(peer)[1], topo.mask(core, peer), len(topo.engines(core, peer))
 
-        def send(name, dst, src, codes, t=t, rid=rid, pid=pid, mask=mask, ne=ne):
+        def send(name, dst, src, codes, sem, rid=rid, pid=pid, mask=mask, ne=ne):
             def call(q):
                 o, i = (ap(dst).bitcast(dt.uint8), ap(src).bitcast(dt.uint8)) if codes else (ap(dst), ap(src))
-                q.remote_dma(o, i, T.sem["arr%d" % t], T.sem.sent, pid, rid, mask)
+                q.remote_dma(o, i, T.sem[sem], T.sem.sent, pid, rid, mask)
             op(name, "G", call, [src], [], "sent", ne)
-        for c, a, e in ch[:-1]:
-            c = "" if c == "A" else c
-            send("sendq%s.%d" % (c, t), v(gq, a, e), v(hq, a, e), True)
-            send("sends%s.%d" % (c, t), v(gs, a, e), v(hs, a, e), False)
-        op("arr.%d" % t, "", None, [], [v(gq), v(gs)], "arr%d" % t, 2 * ne * (len(ch) - 1))
-        for i, (c, a, e) in enumerate(parts("sc")):
-            mm("ms%s.%d" % (c, t), bank(CFG["ms"][i], e - a), v("uq2"), v("us2"), v(zq, a, e), v(zs, a, e))
-            move("sc%s.%d" % (c, t), v("sc", a, e), bank(CFG["ms"][i], e - a))
-        for c, a, e in parts("og"):
-            move("og%s.%d" % (c, t), v("og", a, e), v("sc"), v("lh16", k + a // 16, k + e // 16))
-        for c, a, e in parts("og"):
-            tt("dd%s.%d" % (c, t), v("sw", a, e), v("sc"), v("og", a, e), A.is_gt, v("lh16", R * K + k + a // 16, R * K + k + e // 16))
-        scan("t1.%d" % t, v("t1"), v("c1"), v("sw"))
-        tt("e1.%d" % t, v("e1"), v("t1", 15, C, 16), v("dj", k, k + K), A.mult)
-        tt("e2.%d" % t, v("e2"), v("e1"), v("jb", k, k + K), A.add)
-        move("so.%d" % t, v("so"), v("e2"), on="V")
-        for c, a, e in parts("gsig"):
-            move("gsig%s.%d" % (c, t), v("sig", a, e), v("cnt", 0, C), v("so", a // 16, e // 16))
-        for c, a, e in parts("gnx"):
-            move("gnx%s.%d" % (c, t), v("nxf%d" % (t + 1), a, e), v("nxf%d" % t, 0, C), v("so", a // 16, e // 16))
-        for c, a, e in parts("gpv"):
-            move("gpv%s.%d" % (c, t), v("pvf", a, e), v("sig"), v("po%d" % t, a // 16, e // 16))
-        for c, a, e in parts("scn"):
-            scan("scn%s.%d" % (c, t), v("scn", a, e), v("c2", a, e), v("nxf%d" % (t + 1), a, e))
-            ts("no%s.%d" % (c, t), v("no%d" % (t + 1), a // 16, e // 16), v("scn", a + 15, e, 16), col(4), A.subtract)
-        for c, a, e in parts("scp"):
-            scan("scp%s.%d" % (c, t), v("scp", a, e), v("c2", a, e), v("pvf", a, e))
-            ts("po%s.%d" % (c, t), v("po%d" % (t + 1), a // 16, e // 16), v("scp", a + 15, e, 16), col(4), A.subtract)
-        layer(*ch[-1])
-        for c, qc, qs, a, e, o in [(c, hq, hs, a, e, a) for c, a, e in parts("m")] + [("G", gq, gs, 0, G, C)]:
+
+        def links():
+            for i, (c, a, e) in enumerate(parts("sc")):
+                mm("ms%s.%d" % (c, t), bank(CFG["ms"][i], e - a), v("uq2"), v("us2"), v(zq, a, e), v(zs, a, e))
+                move("sc%s.%d" % (c, t), v("sc", a, e), bank(CFG["ms"][i], e - a))
+            for c, a, e in parts("og"):
+                move("og%s.%d" % (c, t), v("og", a, e), v("sc"), v("lh16", k + a // 16, k + e // 16))
+            for c, a, e in parts("og"):
+                tt("dd%s.%d" % (c, t), v("sw", a, e), v("sc"), v("og", a, e), A.is_gt, v("lh16", R * K + k + a // 16, R * K + k + e // 16))
+            scan("t1.%d" % t, v("t1"), v("c16"), v("sw"))
+            tt("e1.%d" % t, v("e1"), v("t1", 15, C, 16), v("dj", k, k + K), A.mult)
+            tt("e2.%d" % t, v("e2"), v("e1"), v("jb", k, k + K), A.add)
+            move("so.%d" % t, v("so"), v("e2"), on="V")
+            for c, a, e in parts("gsig"):
+                move("gsig%s.%d" % (c, t), v("sig", a, e), v("cnt", 0, C), v("so", a // 16, e // 16))
+            for c, a, e in parts("gnx"):
+                move("gnx%s.%d" % (c, t), v("nxf%d" % (t + 1), a, e), v("nxf%d" % t, 0, C), v("so", a // 16, e // 16))
+            for c, a, e in parts("gpv"):
+                ts("gpv%s.%d" % (c, t), v("pvh", a, e), v("sig"), LOW, A.subtract, off=v("po%d" % t, a // 16, e // 16))
+            for c, a, e in parts("scn"):
+                scan("scn%s.%d" % (c, t), v("scn", a, e), v("c4", a, e), v("nxf%d" % (t + 1), a, e))
+                ts("nq%s.%d" % (c, t), v("nq%d" % (t + 1), a // 4, e // 4), v("scn", a + 3, e, 4), 4.0, A.mult, col(3), A.add)
+            for c, a, e in parts("s4"):
+                scan("s4%s.%d" % (c, t), v("s4", a, e), v("c4", a, e), v("pvh", a, e), DROP)
+                ts("pq%s.%d" % (c, t), v("pq%d" % (t + 1), a // 4, e // 4), v("s4", a + 3, e, 4), 4.0, A.mult, col(4), A.add)
+            if t + 1 < R:
+                scan("s16.%d" % t, v("s16"), v("c16"), v("pvh"), DROP)
+                ts("po.%d" % t, v("po%d" % (t + 1)), v("s16", 15, C, 16), col(5), A.subtract, LOW, A.add)
+        links()
+        layer(CFG["l"][2], *CFG["h"][t][-1])
+        count = {"F": 0, "H": 0}
+        for c, a, e in CFG["send"][t]:
+            s = "F" if e <= far else "H"
+            send("send%sq%s.%d" % (s, c, t), v(fq if s == "F" else gq, a, e), v(zq if s == "F" else hq, a, e), True, "arr%s%d" % (s, t))
+            send("send%ss%s.%d" % (s, c, t), v(fs if s == "F" else gs, a, e), v(zs if s == "F" else hs, a, e), False, "arr%s%d" % (s, t))
+            count[s] += 2 * ne
+        if far:
+            op("arrF.%d" % t, "", None, [], [v(fq, 0, far), v(fs, 0, far)], "arrF%d" % t, count["F"])
+            layer(CFG["lG"], "F", 0, far, fq, fs, fh, gq, gs)
+        if far < G:
+            op("arrH.%d" % t, "", None, [], [v(gq, far), v(gs, far)], "arrH%d" % t, count["H"])
+        for i, (c, qc, qs, a, e, o) in enumerate([(c, hq, hs, a, e, a) for c, a, e in parts("m")] + [("G", gq, gs, 0, G, C)]):
             for b in range(4):
-                s = bank(CFG["m" + c][b], e - a)
+                s = bank(CFG["mG" if i % 2 else "m"][b], e - a)
                 mm("m%s%d.%d" % (c, b, t), s, v("eq", 128 * b, 128 * b + 128), v("es", 128 * b, 128 * b + 128), v(qc, a, e), v(qs, a, e))
-                move("d%s%d.%d" % (c, b, t), v(nxt, W * b + o, W * b + o + e - a), s)
+                move("d%s%d.%d" % (c, b, t), v(nxt, 4 * o + b, 4 * (o + e - a), 4), s)
     store("st_nlo", T.nl[:, 0:C], T["nxf%d" % R][0:128:16, :], v("nxf%d" % R))
     for (c, a, e), b in zip(ch, (6, 7, 5)):
         mm("my" + c, bank(b, e - a), v("vq"), v("vs"), v(zq, a, e), v(zs, a, e))
@@ -310,11 +339,11 @@ def rank_program(g, core, T, topo):
             mark[n] = (s, count[s])
     known = {q: {} for q in order}
     after = {}
-    for t in range(R):
-        n = "arr.%d" % t
-        mark[n] = (ops[n][3], ops[n][4])
-        count[ops[n][3]] = ops[n][4]
-        after[n] = {ops[n][3]: ops[n][4]}
+    for n in ops:
+        if not ops[n][0]:
+            mark[n] = (ops[n][3], ops[n][4])
+            count[ops[n][3]] = ops[n][4]
+            after[n] = {ops[n][3]: ops[n][4]}
     queues = {"V": g.vector, "S": g.scalar, "P": g.tensor, "G": g, "Y": g.sync}
     at = {q: 0 for q in order}
     while any(at[q] < len(order[q]) for q in order):

@@ -13,14 +13,15 @@ def cuts(*at, end=C):
     return tuple(("ABCDEFGH"[i], at[i], at[i + 1]) for i in range(len(at) - 1))
 
 
-CFG = {"g": {0: cuts(128, 256), 1: cuts(64, 128, 256, 352), 2: cuts(64, 128, 256, 352), 3: cuts(32, 64, 192, 320)},
-       "a": {0: cuts(128, 256), 1: cuts(128, 256, 352), 2: cuts(128, 256, 352), 3: cuts(64, 192, 320)},
+CFG = {"g": {0: cuts(128, 256), 1: cuts(64, 128, 256, 352), 2: cuts(64, 128, 256, 352), 3: cuts(48, 96, 208, 320)},
+       "a": {0: cuts(128, 256), 1: cuts(128, 256, 352), 2: cuts(128, 256, 352), 3: cuts(96, 208, 320)},
        "z": {0: cuts(128, 256), 1: cuts(128, 256), 2: cuts(128, 256), 3: cuts(320)},
-       "h": {t: cuts(256) for t in range(R)},
-       "send": {t: cuts(128, end=G) for t in range(R)},
-       "far": {t: 128 for t in range(R)},
-       "split": {"og": cuts(256), "sc": cuts(256), "gsig": cuts(256), "s0": cuts(128), "m": cuts(256)},
-       "l": ((0, 1, 2, 3), (6, 7, 0, 1), (2, 3, 6, 7)), "lG": (2, 3, 6, 7), "ms": (4, 5), "m": (0, 1, 4, 5), "mG": (2, 3, 6, 7)}
+       "far": {0: 128, 1: 128, 2: 128},
+       "h": {t: (256, 448) for t in range(R)}, "m": {t: (256, 448) for t in range(R)},
+       "split": {"og": cuts(256), "dd": cuts(256), "sc": cuts(256), "gsig": cuts(256), "s0": cuts(128)},
+       "n4": "plain", "xa": 0, "n16": 1, "eng": {0: 8, 1: 16, 2: 8},
+       "wa": ("gh", None, None, "wc"),
+       "l": ((0, 1, 2, 3), (2, 3, 6, 7), (2, 3, 6, 7)), "ms": (4, 5), "mb": ((0, 1, 4, 5), (2, 3, 6, 7), (0, 1, 4, 5))}
 
 SCRATCH = {
     "nxi": ("sbuf", [128, W // 16], "int32"), "pri": ("sbuf", [128, R * K], "int32"),
@@ -31,53 +32,64 @@ SCRATCH = {
     "wq": ("sbuf", [128, 512], Q4), "wsc": ("sbuf", [128, 512], U8),
     "et": ("sbuf", [128, 516], "bfloat16"), "ones": ("sbuf", [128, W], "bfloat16"),
     "eq": ("sbuf", [128, 512], Q4), "es": ("sbuf", [128, 512], U8),
-    "pi": ("sbuf", [128, K], "int32"), "p16": ("sbuf", [128, K], "uint16"), "ri": ("sbuf", [128, 4], "int32"),
-    "uoi": ("sbuf", [128, 8], "int32"), "uo": ("sbuf", [128, 8], "uint16"), "col": ("sbuf", [128, 8], "float32"),
-    "cnt": ("sbuf", [128, W], "float32"), "sig": ("sbuf", [128, W], "float32"),
+    "pi": ("sbuf", [128, K + 8], "int32"), "p16": ("sbuf", [128, K + 8], "uint16"), "ri": ("sbuf", [128, 2], "int32"),
+    "col": ("sbuf", [128, 8], "float32"), "drop": ("sbuf", [128, 128], "bfloat16"),
+    "cnt": ("sbuf", [128, W], "float32"), "low": ("sbuf", [128, C], "float32"), "sig": ("sbuf", [128, W], "float32"),
     "f16": ("sbuf", [128, 128], "bfloat16"), "f4": ("sbuf", [128, 128], "bfloat16"),
     "c16": ("sbuf", [128, C], "bfloat16"), "c4": ("sbuf", [128, C], "bfloat16"),
-    "j16": ("sbuf", [128, R * K], "float32"), "jf": ("sbuf", [128, R * K], "float32"), "dj": ("sbuf", [128, R * K], "float32"),
-    "kd": ("sbuf", [128, R * K], "float32"), "jb": ("sbuf", [128, R * K], "float32"),
+    "j16": ("sbuf", [128, R * K], "float32"), "jf": ("sbuf", [128, R * K], "float32"),
     "lh": ("sbuf", [128, 2 * R * K], "float32"), "lh16": ("sbuf", [128, 2 * R * K], "uint16"),
-    "e1": ("sbuf", [128, K], "float32"), "e2": ("sbuf", [128, K], "float32"),
+    "ed": ("sbuf", [128, 3 * R * K], "float32"), "ee": ("sbuf", [128, 3 * K], "float32"),
     "nx16": ("sbuf", [128, W // 16], "uint16"), "n4": ("sbuf", [128, 4 * K], "uint16"),
     "pvf0": ("sbuf", [128, W], "float32"), "nxf0": ("sbuf", [128, W], "float32"),
     "scn": ("sbuf", [128, C], "float32"), "s0": ("sbuf", [128, C], "float32"),
+    "nxh": ("sbuf", [128, C], "float16"), "sn": ("sbuf", [128, C], "float16"),
     "pvh": ("sbuf", [128, C], "float16"), "s4": ("sbuf", [128, C], "float16"), "s16": ("sbuf", [128, C], "float16"),
     "sc": ("sbuf", [128, C], "float32"), "og": ("sbuf", [128, C], "float32"),
-    "sw": ("sbuf", [128, C], "bfloat16"), "t1": ("sbuf", [128, C], "float16"),
+    "sw": ("sbuf", [128, C], "bfloat16"), "t1": ("sbuf", [128, 3 * C + 32], "float16"),
     "so": ("sbuf", [128, K], "uint16"), "yt": ("sbuf", [128, C], "float32"),
 }
 for _t in range(R + 1):
     SCRATCH["win%d" % _t] = ("sbuf", [128, 4 * W], "bfloat16")
     SCRATCH["tmp%d" % _t] = ("sbuf", [128, 4 * C], "bfloat16")
     SCRATCH["z%d" % _t] = ("sbuf", [128, 4 * C], "bfloat16")
-    SCRATCH["zq%d" % _t] = ("sbuf", [128, C], Q4)
-    SCRATCH["zs%d" % _t] = ("sbuf", [128, C], U8)
+    SCRATCH["zq%d" % _t] = ("sbuf", [128, W], Q4)
+    SCRATCH["zs%d" % _t] = ("sbuf", [128, W], U8)
     SCRATCH["pq%d" % _t] = ("sbuf", [128, 4 * K], "uint16")
+    SCRATCH["nq%d" % _t] = ("sbuf", [128, 4 * K], "uint16")
 for _t in range(R):
     SCRATCH["po%d" % _t] = ("sbuf", [128, K], "uint16")
-    SCRATCH["h%d" % _t] = ("sbuf", [128, 4 * C], "bfloat16")
-    SCRATCH["hq%d" % _t] = ("sbuf", [128, C], Q4)
-    SCRATCH["hs%d" % _t] = ("sbuf", [128, C], U8)
-    SCRATCH["gq%d" % _t] = ("sbuf", [128, G], Q4)
-    SCRATCH["gs%d" % _t] = ("sbuf", [128, G], U8)
-    SCRATCH["fq%d" % _t] = ("sbuf", [128, G], Q4)
-    SCRATCH["fs%d" % _t] = ("sbuf", [128, G], U8)
-    SCRATCH["fh%d" % _t] = ("sbuf", [128, 4 * G], "bfloat16")
+    SCRATCH["h%d" % _t] = ("sbuf", [128, 4 * W], "bfloat16")
+    SCRATCH["hq%d" % _t] = ("sbuf", [128, W], Q4)
+    SCRATCH["hs%d" % _t] = ("sbuf", [128, W], U8)
     SCRATCH["nxf%d" % (_t + 1)] = ("sbuf", [128, C], "float32")
-    SCRATCH["nq%d" % (_t + 1)] = ("sbuf", [128, 4 * K], "uint16")
 for _b in range(8):
     SCRATCH["ps%d" % _b] = ("psum", [128, 512], "float32")
 
 LOADS = ["nx", "pr", "x", "gh", "u", "v", "wc", "ws"]
 SEMAPHORES = ["cV", "cS", "cP", "cG", "out", "sent"] + ["ld_" + n for n in LOADS] + ["arr%s%d" % (c, t) for t in range(R) for c in "FH"]
 
-ORDER = {'V': 'f4a ones r2 r0 r1 f16a p16 rf cnt uo k6 nx16 n41 n40 n42 scat n43 s0A gA3.0 pq0A s0B aA.0 pq0B zA.0 aB.0 zB.0 qu dj uq2 aC.0 zC.0 lo qe2 hi qe3 lh16 hA.0 qe0 s1 qe1 ddA.0 ddB.0 rB0.0 t1.0 rB3.0 e1.0 jb hB.0 e2.0 qv so.0 po0 rF0.0 rF3.0 gsigB.0 hF.0 dB2.0 gpv.0 scn.0 s4.0 nq.0 dG1.0 dG2.0 pq.0 gB.1 aA.1 aB.1 zA.1 zB.1 aC.1 aD.1 zC.1 s16.0 scB.1 hA.1 ogB.1 po.0 ddB.1 ddA.1 dA0.1 t1.1 hB.1 e1.1 dA1.1 e2.1 rF2.1 so.1 rF1.1 gsigA.1 hF.1 dB0.1 gpv.1 scn.1 dB2.1 dG0.1 s4.1 nq.1 pq.1 gB.2 aA.2 aB.2 zA.2 zB.2 aD.2 aC.2 zC.2 rA1.2 s16.1 hA.2 ogB.2 rB1.2 ddB.2 ddA.2 rB2.2 t1.2 po.1 e1.2 hB.2 e2.2 rF3.2 so.2 rF0.2 dA2.2 hF.2 dB2.2 dB0.2 gpv.2 scn.2 s4.2 dG2.2 dG1.2 nq.2 pq.2 gB.3 gA.3 aA.3 aB.3 aC.3 zA.3 aD.3 zB.3 yB', 'S': 'ld_gh k3 c4 k4 nxf k5 jf c16 k7 gA0.0 gA1.0 gA2.0 gB2.0 gB0.0 gB3.0 gB1.0 gC2.0 gC3.0 gC0.0 gC1.0 us2 kd rA3.0 rA0.0 rA2.0 scA.0 rA1.0 scB.0 rB2.0 ogA.0 ogB.0 dA3.0 dA2.0 rB1.0 dA0.0 dA1.0 rF1.0 rF2.0 gsigA.0 gnx.0 dB0.0 dB1.0 dB3.0 dG0.0 dG3.0 gA.1 gC.1 gD.1 gE.1 rA0.1 rA2.1 rA1.1 rA3.1 scA.1 rB3.1 ogA.1 rB1.1 rB0.1 rB2.1 dA2.1 dA3.1 rF0.1 rF3.1 gsigB.1 gnx.1 dB3.1 dB1.1 dG1.1 dG3.1 dG2.1 gA.2 gC.2 gE.2 gD.2 rA3.2 rA2.2 rA0.2 scA.2 scB.2 rB3.2 ogA.2 rB0.2 dA3.2 dA0.2 dA1.2 rF1.2 rF2.2 gsigA.2 gsigB.2 gnx.2 dB1.2 dB3.2 dG0.2 dG3.2 gC.3 gD.3 gE.3 yA st_os0 st_os1', 'P': 'lA0.0 lA3.0 lA2.0 msA.0 lA1.0 msB.0 lB2.0 lB0.0 lB3.0 mA3.0 mA2.0 lB1.0 mA1.0 mA0.0 lF1.0 lF0.0 lF2.0 lF3.0 mB1.0 mB0.0 mB2.0 mB3.0 mG0.0 mG1.0 mG3.0 mG2.0 lA0.1 lA2.1 lA1.1 lA3.1 msA.1 msB.1 lB3.1 lB0.1 lB1.1 mA0.1 lB2.1 mA2.1 mA1.1 mA3.1 lF2.1 lF0.1 lF3.1 lF1.1 mB2.1 mB0.1 mB3.1 mB1.1 mG1.1 mG3.1 mG0.1 mG2.1 lA3.2 lA2.2 lA0.2 lA1.2 msA.2 msB.2 lB3.2 lB0.2 lB1.2 mA0.2 mA3.2 mA1.2 lB2.2 lF1.2 lF3.2 lF2.2 lF0.2 mA2.2 mB2.2 mB0.2 mB3.2 mB1.2 mG0.2 mG2.2 mG3.2 mG1.2 myA myB', 'G': 'pi f4b f4c uoi j16 f16b f16c E sigg sendFqA.0 sendFsA.0 sendHqB.0 sendHsB.0 sendFqA.1 sendFsA.1 sendHqB.1 sendHsB.1 sendFqA.2 sendFsA.2 sendHqB.2 sendHsB.2', 'Y': 'ld_nx ld_x ld_pr ld_wc ld_ws ld_u ld_v st_nlg st_nlo st_ocA st_yA st_ocB st_os2 st_os3 st_yB'}
+ORDER = {
+    "V": "f4a ones r2 r0 p16 rf cnt nx16 n40 n43 scat n41 n42 s0A s0B pq0A gA2.0 gA0.0 aA.0 pq0B zA.0 aB.0 qu zB.0 uq2 aC.0 qe3 zC.0 hi lo hA.0 lh16 qe2 qe1 qe0 s1 ddB.0 ddA.0 dj t1.0 hB.0 e1.0 so.0 rC2.0 rC3.0 rC1.0 gsigA.0 hC.0 po0 qv gpv.0 scn.0"
+         " | dC2 dC0 nq s4 gB pq aA aB zA zB aC aD zC rA1 hA s16 ogB rB2 ddB ddA rC1 t1 hB e1 po so hC gsigB dB3 dB1 gpv scn"
+         " | dC3.2 dC0.2 nq.2 s4.2 gB.3 pq.2 aA.3 aB.3 aC.3 zA.3 aD.3 zB.3 yB",
+    "S": "k2 k7 k3 k4 c4 nxf c16 gA1.0 gA3.0 gB1.0 gB3.0 gB2.0 gB0.0 k6 jf gC1.0 gC0.0 gC3.0 gC2.0 us2 cj nxg ck rA0.0 rA3.0 rA2.0 rA1.0 scA.0 k5 scB.0 rB2.0 ogB.0 ogA.0 rB3.0 rB0.0 rB1.0 dA3.0 dA2.0 dA1.0 dA0.0 gsigB.0 rC0.0 gnx.0 dB3.0 dB0.0 dB2.0 dB1.0"
+         " | dC3 dC1 gA gC gD nc gE rA3 rA0 rA2 scA scB rB3 rB1 ogA rB0 dA0 dA2 rC2 dA3 rC0 rC3 dA1 gsigA gnx dB0 dB2"
+         " | dC2.2 dC1.2 gA.3 gC.3 gD.3 gE.3 nc.3 yA st_os0 st_os1",
+    "P": "lA3.0 lA0.0 lA1.0 lA2.0 msA.0 msB.0 lB2.0 lB1.0 mA3.0 lB3.0 lB0.0 mA1.0 mA2.0 mA0.0 lC2.0 lC3.0 lC1.0 lC0.0 mB2.0 mB3.0 mB1.0 mB0.0 mC2.0 mC3.0 mC0.0 mC1.0"
+         " | lA3 lA0 lA2 lA1 msA msB lB3 lB1 lB2 mA2 lB0 mA0 lC1 lC2 mA3 lC0 lC3 mA1 mB1 mB3 mB0 mB2 mC2 mC3 mC0 mC1 | myA myB",
+    "G": "pi uoi f4b f4c j16 f16b f16c E ed sigg sendFq.0 sendFs.0 low sendHq.0 sendHs.0 | sendFq sendFs sendHq sendHs |",
+    "Y": "ld_nx ld_x ld_gh ld_pr ld_wc ld_ws ld_u ld_v st_nlg | | st_ocA st_nlo st_yA st_ocB st_os2 st_os3 st_yB",
+}
+LATE = ("s16", "po", "s4", "pq", "nq", "dC0", "dC1", "dC2", "dC3")
 
 
 def plan():
-    return {q: ORDER[q].split() for q in ORDER}
+    order = {}
+    for q in ORDER:
+        first, each, last = [x.split() for x in ORDER[q].split("|")]
+        order[q] = first + ["%s.%d" % (n, t - (n in LATE)) for t in range(1, R) for n in each] + last
+    return order
 
 
 def meets(a, b):
@@ -116,17 +128,17 @@ def build(core, T, topo, where):
     def arg(x):
         return ap(x) if isinstance(x, tuple) else x
 
-    def ts(name, out, x, s1, o1, s2=None, o2=None, off=None):
+    def ts(name, out, x, s1, o1, s2=None, o2=None):
         if o2 is None:
-            op(name, "V", lambda q: q.tensor_scalar(ap(out), ap(x).indirect(ap(off)) if off else ap(x), arg(s1), None, o1), views(x, s1, off), [out])
+            op(name, "V", lambda q: q.tensor_scalar(ap(out), ap(x), arg(s1), None, o1), views(x, s1), [out])
         else:
             op(name, "V", lambda q: q.tensor_scalar(ap(out), ap(x), arg(s1), arg(s2), o1, o2), views(x, s1, s2), [out])
 
     def tt(name, out, x, y, o, off=None):
         op(name, "V", lambda q: q.tensor_tensor(ap(out), ap(x).indirect(ap(off)) if off else ap(x), ap(y), o), views(x, y, off), [out])
 
-    def act(name, out, x, f, scale=1.0, bias=0.0):
-        op(name, "S", lambda q: q.activation(ap(out), ap(x), f, bias=arg(bias), scale=arg(scale)), views(x, scale, bias), [out])
+    def act(name, out, x, f, scale=1.0, bias=0.0, off=None):
+        op(name, "S", lambda q: q.activation(ap(out), ap(x).indirect(ap(off)) if off else ap(x), f, bias=arg(bias), scale=arg(scale)), views(x, scale, bias, off), [out])
 
     def move(name, out, x, off=None, relu=None, on="SV"):
         def call(q):
@@ -166,58 +178,62 @@ def build(core, T, topo, where):
     def parts(name):
         return CFG["split"].get(name, (("", 0, C),))
 
-    load("nx", v("nxi")); load("pr", v("pri")); load("x", v("win0", 0, 4 * C)); load("gh", v("win0", 4 * C))
-    load("wc", v("wq"), True, v("nxi")); load("ws", v("wsc")); load("u", v("ut")); load("v", v("vt"))
-    iota("pi", v("pi"), [[0, K]], 0, 1, False)
+    iota("pi", v("pi", 0, K), [[0, K]], 0, 1, False)
+    load("nx", v("nxi")); load("pr", v("pri")); load("gh", v("win0", 4 * C))
+    load("x", v("win0", 0, 4 * C), False, v("pi", 0, K) if CFG["xa"] else None)
+    landed = {"nx": v("nxi"), "gh": v("win0", 4 * C), "x": v("win0", 0, 4 * C), "pr": v("pri"), "wc": v("wq"), None: None}
+    wa = [landed[n] for n in CFG["wa"]]
+    load("wc", v("wq"), True, wa[0]); load("ws", v("wsc"), False, wa[1]); load("u", v("ut"), False, wa[2]); load("v", v("vt"), False, wa[3])
     iota("j16", v("j16"), [[0, R], [16, K]], 0, 0)
-    iota("uoi", v("uoi"), [[16, 8]], 0, 0, False)
+    iota("uoi", v("pi", K), [[16, 8]], 0, 0, False)
     fill("ones", v("ones"), 1.0)
     scan("cnt", v("cnt"), v("ones"), v("ones"), -1.0, A.add, A.mult)
     select("E", v("et"), v("ones", 0, 516), [[1, 516]], A.is_equal, 0.0, -3, -4)
     for b in range(4):
         quant("qe%d" % b, v("eq", 128 * b, 128 * b + 128), v("es", 128 * b, 128 * b + 128), v("et", 3 - b, 515 - b))
     move("p16", v("p16"), v("pi"), on="V")
-    fill("f4a", v("f4"), DROP)
-    select("f4b", v("f4"), v("f4"), [[-16, 8], [0, 4], [-4, 4]], A.is_ge, float(W), 0, 1)
+    fill("f4a", v("drop"), DROP)
+    select("f4b", v("f4"), v("drop"), [[-16, 8], [0, 4], [-4, 4]], A.is_ge, float(W), 0, 1)
     select("f4c", v("f4"), v("f4"), [[16, 8], [0, 4], [4, 4]], A.is_ge, float(W), 3, -1)
-    move("c4", v("c4"), v("f4"), v("p16"))
-    fill("f16a", v("f16"), 0.0)
-    select("f16b", v("f16"), v("f16"), [[1, 128]], A.not_equal, DROP, 0, -1)
+    move("c4", v("c4"), v("f4"), v("p16", 0, K))
+    select("f16b", v("f16"), v("drop"), [[1, 128]], A.is_equal, 0.0, 0, -1)
     select("f16c", v("f16"), v("f16"), [[1, 128]], A.not_equal, STEP, -1, -1)
-    move("c16", v("c16"), v("f16"), v("p16"))
+    move("c16", v("c16"), v("f16"), v("p16", 0, K))
     ts("r0", v("ri", 0, 1), v("pi", 0, 1), 15, A.bitwise_and)
-    ts("r1", v("ri", 1, 2), v("pi", 0, 1), 2, A.logical_shift_right, 3, A.bitwise_and)
-    ts("r2", v("ri", 2, 3), v("pi", 0, 1), 3, A.bitwise_and)
-    move("rf", v("col", 0, 3), v("ri", 0, 3), on="V")
-    act("k3", col(7), col(1), F.Identity, 4.0 * W, -12.0 * W)
-    act("k4", col(3), col(7), F.Identity, 1.0, col(2))
+    ts("r2", v("ri", 1, 2), v("pi", 0, 1), 3, A.bitwise_and)
+    move("rf", v("col", 0, 2), v("ri"), on="V")
+    act("k3", col(7), col(0), F.Identity, 1.0 * W, -12.0 * W)
+    act("k4", col(3), col(1), F.Identity, 1.0 - W, col(7))
     act("k5", col(4), col(3), F.Identity, 1.0, 4 * LOW)
-    ts("k6", col(5), col(0), 15.0, A.is_lt, STEP, A.mult)
-    act("k7", col(6), col(5), F.Copy, -1.0)
+    act("k2", col(2), col(0), F.Relu, 1.0, -14.0)
+    act("k6", col(5), col(2), F.Identity, -STEP, STEP)
+    act("k7", col(6), col(2), F.Identity, STEP, -STEP)
     move("nx16", v("nx16"), v("nxi"), on="V")
-    for b in range(4):
-        ts("n4%d" % b, v("n4", K * b, K * b + K), v("nxi", 0, K), 4.0, A.mult, float(b), A.add)
     op("scat", "V", lambda q: q.tensor_copy(ap(v("pvf0")).indirect(ap(v("nx16"))), ap(v("cnt"))), [v("nx16"), v("cnt")], [v("pvf0")])
     for c, a, e in parts("s0"):
-        scan("s0" + c, v("scn", a, e), v("c4", a, e), v("pvf0", a, e))
-        ts("pq0" + c, v("pq0", a // 4, e // 4), v("scn", a + 3, e, 4), 4.0, A.mult, col(3), A.add)
+        scan("s0" + c, v("s0", a, e), v("c4", a, e), v("pvf0", a, e))
+        ts("pq0" + c, v("pq0", a // 4, e // 4), v("s0", a + 3, e, 4), 4.0, A.mult, col(3), A.add)
+    act("nxf", v("nxf0", 0, C), v("cnt"), F.Identity, 1.0, -LOW if CFG.get("n16") else 0.0, v("nx16", 0, K))
+    move("nxg", v("nxf0", C), v("cnt"), v("nx16", K))
+    for b in range(4):
+        ts("n4%d" % b, v("n4", K * b, K * b + K), v("nxi", 0, K), 4.0, A.mult, float(b), A.add)
     scan("s1", v("s0"), v("c16"), v("pvf0", 0, C))
     ts("po0", v("po0"), v("s0", 15, C, 16), col(5), A.subtract)
     act("jf", v("jf"), v("j16"), F.Identity, 1.0, col(0))
-    tt("dj", v("dj"), v("pri"), v("jf"), A.subtract)
+    iota("ed", v("ed"), [[0, R * K], [1, 3]], 0, 0)
+    tt("dj", v("ed", 2, 3 * R * K, 3), v("pri"), v("jf"), A.subtract)
     tt("lo", v("lh", 0, R * K), v("pri"), v("jf"), A.min)
     tt("hi", v("lh", R * K), v("pri"), v("jf"), A.max)
     move("lh16", v("lh16"), v("lh"), on="V")
-    act("kd", v("kd"), v("dj"), F.Identity, col(6))
-    tt("jb", v("jb"), v("kd"), v("jf"), A.add)
-    iota("sigg", v("sig", C), [[1, G]], C, 0)
-    move("nxf", v("nxf0"), v("cnt"), v("nx16"))
+    act("ck", v("t1", 61, 3 * C + 30, 48), v("jf", 0, K), F.Identity, 0.0, col(6))
+    act("cj", v("t1", 77, 3 * C + 30, 48), v("jf", 0, K), F.Copy)
+    iota("low", v("low"), [[1, C]], -int(LOW), 0)
+    iota("sigg", v("sig", C), [[1, G]], C - int(LOW), 0)
     store("st_nlg", T.nl[:, C:W], T.nxf0[0:128:16, C:W], v("nxf0", C))
-    move("uo", v("uo"), v("uoi"), on="V")
     quant("qu", v("uq"), v("us"), v("ut"))
-    op("uq2", "V", lambda q: q.tensor_copy(T.uq2[:, 0:128].bitcast(dt.uint32), T.uq[:, 0:128].bitcast(dt.uint32).indirect(T.uo[:, 0:8])),
-       [v("uq"), v("uo")], [v("uq2")])
-    op("us2", "S", lambda q: q.activation(T.us2[:, 0:128], T.us[:, 0:128].indirect(T.uo[:, 0:8]), F.Copy), [v("us"), v("uo")], [v("us2")])
+    op("uq2", "V", lambda q: q.tensor_copy(T.uq2[:, 0:128].bitcast(dt.uint32), T.uq[:, 0:128].bitcast(dt.uint32).indirect(T.p16[:, K:K + 8])),
+       [v("uq"), v("p16", K)], [v("uq2")])
+    move("us2", v("us2"), v("us"), v("p16", K))
     quant("qv", v("vq"), v("vs"), v("vt"))
 
     for t in range(R + 1):
@@ -235,73 +251,76 @@ def build(core, T, topo, where):
             quant("z%s.%d" % (c, t), v(zq, a, e), v(zs, a, e), v(z, 4 * a, 4 * e))
         if t == R:
             break
-        h, hq, hs, gq, gs, nxt = "h%d" % t, "hq%d" % t, "hs%d" % t, "gq%d" % t, "gs%d" % t, "win%d" % (t + 1)
-        fq, fs, fh, far = "fq%d" % t, "fs%d" % t, "fh%d" % t, CFG["far"][t]
-        k = K * t
-
-        def layer(banks, c, a, e, zq=zq, zs=zs, h=h, hq=hq, hs=hs):
-            for b in range(4):
-                s = bank(banks[b], e - a)
-                mm("l%s%d.%d" % (c, b, t), s, v("wq", 128 * b, 128 * b + 128), v("wsc", 128 * b, 128 * b + 128), v(zq, a, e), v(zs, a, e))
-                move("r%s%d.%d" % (c, b, t), v(h, 4 * a + b, 4 * e, 4), s, relu=0.015625)
-            quant("h%s.%d" % (c, t), v(hq, a, e), v(hs, a, e), v(h, 4 * a, 4 * e))
-        for i, x in enumerate(CFG["h"][t][:-1]):
-            layer(CFG["l"][i], *x)
+        h, hq, hs, nxt, far, k = "h%d" % t, "hq%d" % t, "hs%d" % t, "win%d" % (t + 1), CFG["far"][t], K * t
         peer = T.cores[rank ^ (1 << t % 2)]
         assert topo.may_write(core, peer)
-        rid, pid, mask, ne = topo.addr(peer)[0], topo.addr(peer)[1], topo.mask(core, peer), len(topo.engines(core, peer))
+        used = topo.engines(core, peer)[:CFG["eng"][t]]
+        rid, pid, mask, ne = topo.addr(peer)[0], topo.addr(peer)[1], sum(1 << e for e in used), len(used)
 
-        def send(name, dst, src, codes, sem, rid=rid, pid=pid, mask=mask, ne=ne):
-            def call(q):
-                o, i = (ap(dst).bitcast(dt.uint8), ap(src).bitcast(dt.uint8)) if codes else (ap(dst), ap(src))
-                q.remote_dma(o, i, T.sem[sem], T.sem.sent, pid, rid, mask)
-            op(name, "G", call, [src], [], "sent", ne)
+        def send(s, qc, qs, a, e, t=t, rid=rid, pid=pid, mask=mask, ne=ne):
+            sem = "arr%s%d" % (s, t)
 
-        def links():
-            for i, (c, a, e) in enumerate(parts("sc")):
-                mm("ms%s.%d" % (c, t), bank(CFG["ms"][i], e - a), v("uq2"), v("us2"), v(zq, a, e), v(zs, a, e))
-                move("sc%s.%d" % (c, t), v("sc", a, e), bank(CFG["ms"][i], e - a))
-            for c, a, e in parts("og"):
-                move("og%s.%d" % (c, t), v("og", a, e), v("sc"), v("lh16", k + a // 16, k + e // 16))
-            for c, a, e in parts("og"):
-                tt("dd%s.%d" % (c, t), v("sw", a, e), v("sc"), v("og", a, e), A.is_gt, v("lh16", R * K + k + a // 16, R * K + k + e // 16))
-            scan("t1.%d" % t, v("t1"), v("c16"), v("sw"))
-            tt("e1.%d" % t, v("e1"), v("t1", 15, C, 16), v("dj", k, k + K), A.mult)
-            tt("e2.%d" % t, v("e2"), v("e1"), v("jb", k, k + K), A.add)
-            move("so.%d" % t, v("so"), v("e2"), on="V")
-            for c, a, e in parts("gsig"):
-                move("gsig%s.%d" % (c, t), v("sig", a, e), v("cnt", 0, C), v("so", a // 16, e // 16))
-            for c, a, e in parts("gnx"):
-                move("gnx%s.%d" % (c, t), v("nxf%d" % (t + 1), a, e), v("nxf%d" % t, 0, C), v("so", a // 16, e // 16))
-            for c, a, e in parts("gpv"):
-                ts("gpv%s.%d" % (c, t), v("pvh", a, e), v("sig"), LOW, A.subtract, off=v("po%d" % t, a // 16, e // 16))
-            for c, a, e in parts("scn"):
-                scan("scn%s.%d" % (c, t), v("scn", a, e), v("c4", a, e), v("nxf%d" % (t + 1), a, e))
-                ts("nq%s.%d" % (c, t), v("nq%d" % (t + 1), a // 4, e // 4), v("scn", a + 3, e, 4), 4.0, A.mult, col(3), A.add)
-            for c, a, e in parts("s4"):
-                scan("s4%s.%d" % (c, t), v("s4", a, e), v("c4", a, e), v("pvh", a, e), DROP)
-                ts("pq%s.%d" % (c, t), v("pq%d" % (t + 1), a // 4, e // 4), v("s4", a + 3, e, 4), 4.0, A.mult, col(4), A.add)
-            if t + 1 < R:
-                scan("s16.%d" % t, v("s16"), v("c16"), v("pvh"), DROP)
-                ts("po.%d" % t, v("po%d" % (t + 1)), v("s16", 15, C, 16), col(5), A.subtract, LOW, A.add)
-        links()
-        layer(CFG["l"][2], *CFG["h"][t][-1])
-        count = {"F": 0, "H": 0}
-        for c, a, e in CFG["send"][t]:
-            s = "F" if e <= far else "H"
-            send("send%sq%s.%d" % (s, c, t), v(fq if s == "F" else gq, a, e), v(zq if s == "F" else hq, a, e), True, "arr%s%d" % (s, t))
-            send("send%ss%s.%d" % (s, c, t), v(fs if s == "F" else gs, a, e), v(zs if s == "F" else hs, a, e), False, "arr%s%d" % (s, t))
-            count[s] += 2 * ne
+            def codes(q):
+                q.remote_dma(ap(v(qc, C + a, C + e)).bitcast(dt.uint8), ap(v(qc, a, e)).bitcast(dt.uint8), T.sem[sem], T.sem.sent, pid, rid, mask)
+
+            def scales(q):
+                q.remote_dma(ap(v(qs, C + a, C + e)), ap(v(qs, a, e)), T.sem[sem], T.sem.sent, pid, rid, mask)
+            op("send%sq.%d" % (s, t), "G", codes, [v(qc, a, e)], [], "sent", ne)
+            op("send%ss.%d" % (s, t), "G", scales, [v(qs, a, e)], [], "sent", ne)
+            op("arr%s.%d" % (s, t), "", None, [], [v(qc, C + a, C + e), v(qs, C + a, C + e)], sem, 2 * ne)
+
+        def layer(ghosts):
+            for i, (c, a, e) in enumerate(cuts(*CFG["h"][t], end=C + far)):
+                if (a >= C) == ghosts:
+                    for b in range(4):
+                        s = bank(CFG["l"][i][b], e - a)
+                        mm("l%s%d.%d" % (c, b, t), s, v("wq", 128 * b, 128 * b + 128), v("wsc", 128 * b, 128 * b + 128), v(zq, a, e), v(zs, a, e))
+                        move("r%s%d.%d" % (c, b, t), v(h, 4 * a + b, 4 * e, 4), s, relu=0.015625)
+                    quant("h%s.%d" % (c, t), v(hq, a, e), v(hs, a, e), v(h, 4 * a, 4 * e))
+
+        def unpack(ghosts):
+            for i, (c, a, e) in enumerate(cuts(*CFG["m"][t], end=W)):
+                if (e > C) == ghosts:
+                    for b in range(4):
+                        s = bank(CFG["mb"][i][b], e - a)
+                        mm("m%s%d.%d" % (c, b, t), s, v("eq", 128 * b, 128 * b + 128), v("es", 128 * b, 128 * b + 128), v(hq, a, e), v(hs, a, e))
+                        move("d%s%d.%d" % (c, b, t), v(nxt, 4 * a + b, 4 * e, 4), s)
+
         if far:
-            op("arrF.%d" % t, "", None, [], [v(fq, 0, far), v(fs, 0, far)], "arrF%d" % t, count["F"])
-            layer(CFG["lG"], "F", 0, far, fq, fs, fh, gq, gs)
+            send("F", zq, zs, 0, far)
+        for i, (c, a, e) in enumerate(parts("sc")):
+            mm("ms%s.%d" % (c, t), bank(CFG["ms"][i], e - a), v("uq2"), v("us2"), v(zq, a, e), v(zs, a, e))
+            move("sc%s.%d" % (c, t), v("sc", a, e), bank(CFG["ms"][i], e - a))
+        layer(False)
         if far < G:
-            op("arrH.%d" % t, "", None, [], [v(gq, far), v(gs, far)], "arrH%d" % t, count["H"])
-        for i, (c, qc, qs, a, e, o) in enumerate([(c, hq, hs, a, e, a) for c, a, e in parts("m")] + [("G", gq, gs, 0, G, C)]):
-            for b in range(4):
-                s = bank(CFG["mG" if i % 2 else "m"][b], e - a)
-                mm("m%s%d.%d" % (c, b, t), s, v("eq", 128 * b, 128 * b + 128), v("es", 128 * b, 128 * b + 128), v(qc, a, e), v(qs, a, e))
-                move("d%s%d.%d" % (c, b, t), v(nxt, 4 * o + b, 4 * (o + e - a), 4), s)
+            send("H", hq, hs, far, G)
+        for c, a, e in parts("og"):
+            move("og%s.%d" % (c, t), v("og", a, e), v("sc"), v("lh16", k + a // 16, k + e // 16))
+        for c, a, e in parts("dd"):
+            tt("dd%s.%d" % (c, t), v("sw", a, e), v("sc"), v("og", a, e), A.is_gt, v("lh16", R * K + k + a // 16, R * K + k + e // 16))
+        scan("t1.%d" % t, v("t1", 0, 3 * C, 3), v("c16"), v("sw"))
+        scan("e1.%d" % t, v("ee"), v("ed", 3 * k, 3 * (k + K)), v("t1", 45, 3 * C + 30, 16), 0.0, A.mult, A.add)
+        move("so.%d" % t, v("so"), v("ee", 2, 3 * K, 3), on="V")
+        for c, a, e in parts("gsig"):
+            move("gsig%s.%d" % (c, t), v("sig", a, e), v("low"), v("so", a // 16, e // 16))
+        move("gnx.%d" % t, v("nxh" if CFG.get("n16") else "nxf%d" % (t + 1)), v("nxf%d" % t, 0, C), v("so"))
+        for c, a, e in parts("gpv"):
+            move("gpv%s.%d" % (c, t), v("pvh", a, e), v("sig"), v("po%d" % t, a // 16, e // 16))
+        if CFG.get("n16"):
+            scan("scn.%d" % t, v("sn"), v("c4"), v("nxh"), DROP)
+            ts("nq.%d" % t, v("nq%d" % (t + 1)), v("sn", 3, C, 4), 4.0, A.mult, col(4), A.add)
+            act("nc.%d" % (t + 1), v("nxf%d" % (t + 1)), v("nxh"), F.Identity, 1.0, LOW if t + 1 == R else 0.0)
+        else:
+            scan("scn.%d" % t, v("scn"), v("c4"), v("nxf%d" % (t + 1)))
+            ts("nq.%d" % t, v("nq%d" % (t + 1)), v("scn", 3, C, 4), 4.0, A.mult, col(3), A.add)
+        scan("s4.%d" % t, v("s4"), v("c4"), v("pvh"), DROP)
+        ts("pq.%d" % t, v("pq%d" % (t + 1)), v("s4", 3, C, 4), 4.0, A.mult, col(4), A.add)
+        if t + 1 < R:
+            scan("s16.%d" % t, v("s16"), v("c16"), v("pvh"), DROP)
+            ts("po.%d" % t, v("po%d" % (t + 1)), v("s16", 15, C, 16), col(5), A.subtract, LOW, A.add)
+        layer(True)
+        unpack(False)
+        unpack(True)
     store("st_nlo", T.nl[:, 0:C], T["nxf%d" % R][0:128:16, :], v("nxf%d" % R))
     for (c, a, e), b in zip(ch, (6, 7, 5)):
         mm("my" + c, bank(b, e - a), v("vq"), v("vs"), v(zq, a, e), v(zs, a, e))
@@ -309,7 +328,7 @@ def build(core, T, topo, where):
         store("st_oc" + c, T.oc[:, 4 * a:4 * e], ap(v(zq, a, e)).bitcast(dt.uint8), v(zq, a, e))
         store("st_y" + c, T.y[:, a:e], ap(v("yt", a, e)), v("yt", a, e))
     for i in range(4):
-        store("st_os%d" % i, T.osc[4 * i:4 * i + 4, :], T[zs][32 * i:32 * i + 4, :], v(zs))
+        store("st_os%d" % i, T.osc[4 * i:4 * i + 4, :], T[zs][32 * i:32 * i + 4, 0:C], v(zs, 0, C))
     return ops
 
 

from concourse.mybir import dt, AluOpType, ActivationFunctionType

C, G, R = 448, 256, 3
W = C + G
K = C // 16
Q4, U8 = "float8_e4m3fn_x4", "uint8"
STEP, DROP = 1024.0, -4096.0
LOW = 2.0 * W


def cuts(*at, end=C):
    at = (0,) + at + (end,)
    return tuple(("ABCDEFGH"[i], at[i], at[i + 1]) for i in range(len(at) - 1))


CFG = {"g": {0: cuts(128, 256), 1: cuts(64, 128, 256, 352), 2: cuts(64, 128, 256, 352), 3: cuts(48, 96, 208, 320)},
       "a": {0: cuts(128, 256), 1: cuts(128, 256, 352), 2: cuts(128, 256, 352), 3: cuts(96, 208, 320)},
       "z": {0: cuts(128, 256), 1: cuts(128, 256), 2: cuts(128, 256), 3: cuts(320)},
       "far": {0: 128, 1: 128, 2: 128},
       "h": {t: (256, 448) for t in range(R)}, "m": {t: (256, 448) for t in range(R)},
       "split": {"og": cuts(256), "dd": cuts(256), "sc": cuts(256), "gsig": cuts(256), "s0": cuts(128)},
       "n4": "plain", "xa": 0, "n16": 1, "eng": {0: 8, 1: 16, 2: 8},
       "wa": ("gh", None, None, "wc"),
       "l": ((0, 1, 2, 3), (2, 3, 6, 7), (2, 3, 6, 7)), "ms": (4, 5), "mb": ((0, 1, 4, 5), (2, 3, 6, 7), (0, 1, 4, 5))}

SCRATCH = {
    "nxi": ("sbuf", [128, W // 16], "int32"), "pri": ("sbuf", [128, R * K], "int32"),
    "ut": ("sbuf", [128, 512], "bfloat16"), "vt": ("sbuf", [128, 512], "bfloat16"),
    "uq": ("sbuf", [128, 128], Q4), "us": ("sbuf", [128, 128], U8),
    "uq2": ("sbuf", [128, 128], Q4), "us2": ("sbuf", [128, 128], U8),
    "vq": ("sbuf", [128, 128], Q4), "vs": ("sbuf", [128, 128], U8),
    "wq": ("sbuf", [128, 512], Q4), "wsc": ("sbuf", [128, 512], U8),
    "et": ("sbuf", [128, 516], "bfloat16"), "ones": ("sbuf", [128, W], "bfloat16"),
    "eq": ("sbuf", [128, 512], Q4), "es": ("sbuf", [128, 512], U8),
    "pi": ("sbuf", [128, K + 8], "int32"), "p16": ("sbuf", [128, K + 8], "uint16"), "ri": ("sbuf", [128, 2], "int32"),
    "col": ("sbuf", [128, 8], "float32"), "drop": ("sbuf", [128, 128], "bfloat16"),
    "cnt": ("sbuf", [128, W], "float32"), "low": ("sbuf", [128, C], "float32"), "sig": ("sbuf", [128, W], "float32"),
    "f16": ("sbuf", [128, 128], "bfloat16"), "f4": ("sbuf", [128, 128], "bfloat16"),
    "c16": ("sbuf", [128, C], "bfloat16"), "c4": ("sbuf", [128, C], "bfloat16"),
    "j16": ("sbuf", [128, R * K], "float32"), "jf": ("sbuf", [128, R * K], "float32"),
    "lh": ("sbuf", [128, 2 * R * K], "float32"), "lh16": ("sbuf", [128, 2 * R * K], "uint16"),
    "ed": ("sbuf", [128, 3 * R * K], "float32"), "ee": ("sbuf", [128, 3 * K], "float32"),
    "nx16": ("sbuf", [128, W // 16], "uint16"), "n4": ("sbuf", [128, 4 * K], "uint16"),
    "pvf0": ("sbuf", [128, W], "float32"), "nxf0": ("sbuf", [128, W], "float32"),
    "scn": ("sbuf", [128, C], "float32"), "s0": ("sbuf", [128, C], "float32"),
    "nxh": ("sbuf", [128, C], "float16"), "sn": ("sbuf", [128, C], "float16"),
    "pvh": ("sbuf", [128, C], "float16"), "s4": ("sbuf", [128, C], "float16"), "s16": ("sbuf", [128, C], "float16"),
    "sc": ("sbuf", [128, C], "float32"), "og": ("sbuf", [128, C], "float32"),
    "sw": ("sbuf", [128, C], "bfloat16"), "t1": ("sbuf", [128, 3 * C + 32], "float16"),
    "so": ("sbuf", [128, K], "uint16"), "yt": ("sbuf", [128, C], "float32"),
}
for _t in range(R + 1):
    SCRATCH["win%d" % _t] = ("sbuf", [128, 4 * W], "bfloat16")
    SCRATCH["tmp%d" % _t] = ("sbuf", [128, 4 * C], "bfloat16")
    SCRATCH["z%d" % _t] = ("sbuf", [128, 4 * C], "bfloat16")
    SCRATCH["zq%d" % _t] = ("sbuf", [128, W], Q4)
    SCRATCH["zs%d" % _t] = ("sbuf", [128, W], U8)
    SCRATCH["pq%d" % _t] = ("sbuf", [128, 4 * K], "uint16")
    SCRATCH["nq%d" % _t] = ("sbuf", [128, 4 * K], "uint16")
for _t in range(R):
    SCRATCH["po%d" % _t] = ("sbuf", [128, K], "uint16")
    SCRATCH["h%d" % _t] = ("sbuf", [128, 4 * W], "bfloat16")
    SCRATCH["hq%d" % _t] = ("sbuf", [128, W], Q4)
    SCRATCH["hs%d" % _t] = ("sbuf", [128, W], U8)
    SCRATCH["nxf%d" % (_t + 1)] = ("sbuf", [128, C], "float32")
for _b in range(8):
    SCRATCH["ps%d" % _b] = ("psum", [128, 512], "float32")

LOADS = ["nx", "pr", "x", "gh", "u", "v", "wc", "ws"]
SEMAPHORES = ["cV", "cS", "cP", "cG", "out", "sent"] + ["ld_" + n for n in LOADS] + ["arr%s%d" % (c, t) for t in range(R) for c in "FH"]

ORDER = {
    "V": "f4a ones r2 r0 p16 rf cnt nx16 n40 n43 scat n41 n42 s0A s0B pq0A gA2.0 gA0.0 aA.0 pq0B zA.0 aB.0 qu zB.0 uq2 aC.0 qe3 zC.0 hi lo hA.0 lh16 qe2 qe1 qe0 s1 ddB.0 ddA.0 dj t1.0 hB.0 e1.0 so.0 rC2.0 rC3.0 rC1.0 gsigA.0 hC.0 po0 qv gpv.0 scn.0"
         " | dC2 dC0 nq s4 gB pq aA aB zA zB aC aD zC rA1 hA s16 ogB rB2 ddB ddA rC1 t1 hB e1 po so hC gsigB dB3 dB1 gpv scn"
         " | dC3.2 dC0.2 nq.2 s4.2 gB.3 pq.2 aA.3 aB.3 aC.3 zA.3 aD.3 zB.3 yB",
    "S": "k2 k7 k3 k4 c4 nxf c16 gA1.0 gA3.0 gB1.0 gB3.0 gB2.0 gB0.0 k6 jf gC1.0 gC0.0 gC3.0 gC2.0 us2 cj nxg ck rA0.0 rA3.0 rA2.0 rA1.0 scA.0 k5 scB.0 rB2.0 ogB.0 ogA.0 rB3.0 rB0.0 rB1.0 dA3.0 dA2.0 dA1.0 dA0.0 gsigB.0 rC0.0 gnx.0 dB3.0 dB0.0 dB2.0 dB1.0"
         " | dC3 dC1 gA gC gD nc gE rA3 rA0 rA2 scA scB rB3 rB1 ogA rB0 dA0 dA2 rC2 dA3 rC0 rC3 dA1 gsigA gnx dB0 dB2"
         " | dC2.2 dC1.2 gA.3 gC.3 gD.3 gE.3 nc.3 yA st_os0 st_os1",
    "P": "lA3.0 lA0.0 lA1.0 lA2.0 msA.0 msB.0 lB2.0 lB1.0 mA3.0 lB3.0 lB0.0 mA1.0 mA2.0 mA0.0 lC2.0 lC3.0 lC1.0 lC0.0 mB2.0 mB3.0 mB1.0 mB0.0 mC2.0 mC3.0 mC0.0 mC1.0"
         " | lA3 lA0 lA2 lA1 msA msB lB3 lB1 lB2 mA2 lB0 mA0 lC1 lC2 mA3 lC0 lC3 mA1 mB1 mB3 mB0 mB2 mC2 mC3 mC0 mC1 | myA myB",
    "G": "pi uoi f4b f4c j16 f16b f16c E ed sigg sendFq.0 sendFs.0 low sendHq.0 sendHs.0 | sendFq sendFs sendHq sendHs |",
    "Y": "ld_nx ld_x ld_gh ld_pr ld_wc ld_ws ld_u ld_v st_nlg | | st_ocA st_nlo st_yA st_ocB st_os2 st_os3 st_yB",
}
LATE = ("s16", "po", "s4", "pq", "nq", "dC0", "dC1", "dC2", "dC3")


def plan():
    order = {}
    for q in ORDER:
        first, each, last = [x.split() for x in ORDER[q].split("|")]
        order[q] = first + ["%s.%d" % (n, t - (n in LATE)) for t in range(1, R) for n in each] + last
    return order


def meets(a, b):
    if a[0] != b[0]:
        return False
    if a[0].startswith("ps"):
        return True
    if a[1] >= b[2] or b[1] >= a[2]:
        return False
    return not (a[3] == b[3] and (a[1] - b[1]) % a[3])


def build(core, T, topo, where):
    rank = T.rank_of(core)
    A, F = AluOpType, ActivationFunctionType
    ops = {}

    def v(name, a=0, b=None, s=1):
        return (name, a, SCRATCH[name][1][1] if b is None else b, s)

    def ap(x):
        return T[x[0]][:, x[1]:x[2]:x[3]] if x[3] > 1 else T[x[0]][:, x[1]:x[2]]

    def op(name, on, call, reads, writes, sem=None, n=1):
        ops[name] = (call, reads, writes, sem, n, on)

    def bank(b, n):
        return ("ps%d" % b, 0, n, 1)

    def col(i):
        return v("col", i, i + 1)

    def views(*xs):
        return [x for x in xs if isinstance(x, tuple)]

    def arg(x):
        return ap(x) if isinstance(x, tuple) else x

    def ts(name, out, x, s1, o1, s2=None, o2=None):
        if o2 is None:
            op(name, "V", lambda q: q.tensor_scalar(ap(out), ap(x), arg(s1), None, o1), views(x, s1), [out])
        else:
            op(name, "V", lambda q: q.tensor_scalar(ap(out), ap(x), arg(s1), arg(s2), o1, o2), views(x, s1, s2), [out])

    def tt(name, out, x, y, o, off=None):
        op(name, "V", lambda q: q.tensor_tensor(ap(out), ap(x).indirect(ap(off)) if off else ap(x), ap(y), o), views(x, y, off), [out])

    def act(name, out, x, f, scale=1.0, bias=0.0, off=None):
        op(name, "S", lambda q: q.activation(ap(out), ap(x).indirect(ap(off)) if off else ap(x), f, bias=arg(bias), scale=arg(scale)), views(x, scale, bias, off), [out])

    def move(name, out, x, off=None, relu=None, on="SV"):
        def call(q):
            src = ap(x).indirect(ap(off)) if off else ap(x)
            if where[name] == "S":
                return q.activation(ap(out), src, F.Relu, scale=relu) if relu else q.activation(ap(out), src, F.Copy)
            return q.tensor_scalar(ap(out), src, 0.0, relu, A.max, A.mult) if relu else q.tensor_copy(ap(out), src)
        op(name, on, call, views(x, off), [out])

    def fill(name, out, c):
        op(name, "V", lambda q: q.memset(ap(out), c), [], [out])

    def quant(name, qc, qs, x):
        op(name, "V", lambda q: q.quantize_mx(ap(qc), ap(qs), ap(x)), [x], [qc, qs])

    def mm(name, out, lc, ls, rc, rs):
        op(name, "P", lambda q: q.matmul_mx(ap(out), ap(lc), ap(ls), ap(rc), ap(rs), True, True), [lc, ls, rc, rs], [out])

    def scan(name, out, c, x, first=0.0, o0=A.add, o1=A.max):
        op(name, "V", lambda q: q.tensor_tensor_scan(ap(out), ap(c), ap(x), first, o0, o1), [c, x], [out])

    def iota(name, out, pattern, base, mult, small=True):
        if small:
            op(name, "G", lambda q: q.iota(ap(out), pattern, base, mult, allow_small_or_imprecise_dtypes=True), [], [out])
        else:
            op(name, "G", lambda q: q.iota(ap(out), pattern, base, mult), [], [out])

    def select(name, out, x, pattern, o, other, base, mult):
        op(name, "G", lambda q: q.affine_select(ap(out), ap(x), pattern, o, other, base, mult), [x], [out])

    def load(name, out, codes=False, after=None):
        op("ld_" + name, "YS", lambda q: q.dma_start(ap(out).bitcast(dt.uint8) if codes else ap(out), T[name][:]), views(after), [out], "ld_" + name, 16)

    def store(name, dst, src, x):
        op(name, "YS", lambda q: q.dma_start(dst, src), [x], [], "out", 16)

    def parts(name):
        return CFG["split"].get(name, (("", 0, C),))

    iota("pi", v("pi", 0, K), [[0, K]], 0, 1, False)
    load("nx", v("nxi")); load("pr", v("pri")); load("gh", v("win0", 4 * C))
    load("x", v("win0", 0, 4 * C), False, v("pi", 0, K) if CFG["xa"] else None)
    landed = {"nx": v("nxi"), "gh": v("win0", 4 * C), "x": v("win0", 0, 4 * C), "pr": v("pri"), "wc": v("wq"), None: None}
    wa = [landed[n] for n in CFG["wa"]]
    load("wc", v("wq"), True, wa[0]); load("ws", v("wsc"), False, wa[1]); load("u", v("ut"), False, wa[2]); load("v", v("vt"), False, wa[3])
    iota("j16", v("j16"), [[0, R], [16, K]], 0, 0)
    iota("uoi", v("pi", K), [[16, 8]], 0, 0, False)
    fill("ones", v("ones"), 1.0)
    scan("cnt", v("cnt"), v("ones"), v("ones"), -1.0, A.add, A.mult)
    select("E", v("et"), v("ones", 0, 516), [[1, 516]], A.is_equal, 0.0, -3, -4)
    for b in range(4):
        quant("qe%d" % b, v("eq", 128 * b, 128 * b + 128), v("es", 128 * b, 128 * b + 128), v("et", 3 - b, 515 - b))
    move("p16", v("p16"), v("pi"), on="V")
    fill("f4a", v("drop"), DROP)
    select("f4b", v("f4"), v("drop"), [[-16, 8], [0, 4], [-4, 4]], A.is_ge, float(W), 0, 1)
    select("f4c", v("f4"), v("f4"), [[16, 8], [0, 4], [4, 4]], A.is_ge, float(W), 3, -1)
    move("c4", v("c4"), v("f4"), v("p16", 0, K))
    select("f16b", v("f16"), v("drop"), [[1, 128]], A.is_equal, 0.0, 0, -1)
    select("f16c", v("f16"), v("f16"), [[1, 128]], A.not_equal, STEP, -1, -1)
    move("c16", v("c16"), v("f16"), v("p16", 0, K))
    ts("r0", v("ri", 0, 1), v("pi", 0, 1), 15, A.bitwise_and)
    ts("r2", v("ri", 1, 2), v("pi", 0, 1), 3, A.bitwise_and)
    move("rf", v("col", 0, 2), v("ri"), on="V")
    act("k3", col(7), col(0), F.Identity, 1.0 * W, -12.0 * W)
    act("k4", col(3), col(1), F.Identity, 1.0 - W, col(7))
    act("k5", col(4), col(3), F.Identity, 1.0, 4 * LOW)
    act("k2", col(2), col(0), F.Relu, 1.0, -14.0)
    act("k6", col(5), col(2), F.Identity, -STEP, STEP)
    act("k7", col(6), col(2), F.Identity, STEP, -STEP)
    move("nx16", v("nx16"), v("nxi"), on="V")
    op("scat", "V", lambda q: q.tensor_copy(ap(v("pvf0")).indirect(ap(v("nx16"))), ap(v("cnt"))), [v("nx16"), v("cnt")], [v("pvf0")])
    for c, a, e in parts("s0"):
        scan("s0" + c, v("s0", a, e), v("c4", a, e), v("pvf0", a, e))
        ts("pq0" + c, v("pq0", a // 4, e // 4), v("s0", a + 3, e, 4), 4.0, A.mult, col(3), A.add)
    act("nxf", v("nxf0", 0, C), v("cnt"), F.Identity, 1.0, -LOW if CFG.get("n16") else 0.0, v("nx16", 0, K))
    move("nxg", v("nxf0", C), v("cnt"), v("nx16", K))
    for b in range(4):
        ts("n4%d" % b, v("n4", K * b, K * b + K), v("nxi", 0, K), 4.0, A.mult, float(b), A.add)
    scan("s1", v("s0"), v("c16"), v("pvf0", 0, C))
    ts("po0", v("po0"), v("s0", 15, C, 16), col(5), A.subtract)
    act("jf", v("jf"), v("j16"), F.Identity, 1.0, col(0))
    iota("ed", v("ed"), [[0, R * K], [1, 3]], 0, 0)
    tt("dj", v("ed", 2, 3 * R * K, 3), v("pri"), v("jf"), A.subtract)
    tt("lo", v("lh", 0, R * K), v("pri"), v("jf"), A.min)
    tt("hi", v("lh", R * K), v("pri"), v("jf"), A.max)
    move("lh16", v("lh16"), v("lh"), on="V")
    act("ck", v("t1", 61, 3 * C + 30, 48), v("jf", 0, K), F.Identity, 0.0, col(6))
    act("cj", v("t1", 77, 3 * C + 30, 48), v("jf", 0, K), F.Copy)
    iota("low", v("low"), [[1, C]], -int(LOW), 0)
    iota("sigg", v("sig", C), [[1, G]], C - int(LOW), 0)
    store("st_nlg", T.nl[:, C:W], T.nxf0[0:128:16, C:W], v("nxf0", C))
    quant("qu", v("uq"), v("us"), v("ut"))
    op("uq2", "V", lambda q: q.tensor_copy(T.uq2[:, 0:128].bitcast(dt.uint32), T.uq[:, 0:128].bitcast(dt.uint32).indirect(T.p16[:, K:K + 8])),
       [v("uq"), v("p16", K)], [v("uq2")])
    move("us2", v("us2"), v("us"), v("p16", K))
    quant("qv", v("vq"), v("vs"), v("vt"))

    for t in range(R + 1):
        win, tmp, z, zq, zs = "win%d" % t, "tmp%d" % t, "z%d" % t, "zq%d" % t, "zs%d" % t
        for c, a, e in CFG["g"][t]:
            if t == 0:
                for b in range(4):
                    move("g%s%d.0" % (c, b), v(tmp, 4 * a + b, 4 * e, 4), v(win), v("n4", K * b + a // 16, K * b + e // 16))
            else:
                move("g%s.%d" % (c, t), v(tmp, 4 * a, 4 * e), v(win), v("nq%d" % t, a // 4, e // 4))
        for c, a, e in CFG["a"][t]:
            tt("a%s.%d" % (c, t), v(z, 4 * a, 4 * e), v(win), v(tmp, 4 * a, 4 * e), A.add, v("pq%d" % t, a // 4, e // 4))
        ch = CFG["z"][t]
        for c, a, e in ch:
            quant("z%s.%d" % (c, t), v(zq, a, e), v(zs, a, e), v(z, 4 * a, 4 * e))
        if t == R:
            break
        h, hq, hs, nxt, far, k = "h%d" % t, "hq%d" % t, "hs%d" % t, "win%d" % (t + 1), CFG["far"][t], K * t
        peer = T.cores[rank ^ (1 << t % 2)]
        assert topo.may_write(core, peer)
        used = topo.engines(core, peer)[:CFG["eng"][t]]
        rid, pid, mask, ne = topo.addr(peer)[0], topo.addr(peer)[1], sum(1 << e for e in used), len(used)

        def send(s, qc, qs, a, e, t=t, rid=rid, pid=pid, mask=mask, ne=ne):
            sem = "arr%s%d" % (s, t)

            def codes(q):
                q.remote_dma(ap(v(qc, C + a, C + e)).bitcast(dt.uint8), ap(v(qc, a, e)).bitcast(dt.uint8), T.sem[sem], T.sem.sent, pid, rid, mask)

            def scales(q):
                q.remote_dma(ap(v(qs, C + a, C + e)), ap(v(qs, a, e)), T.sem[sem], T.sem.sent, pid, rid, mask)
            op("send%sq.%d" % (s, t), "G", codes, [v(qc, a, e)], [], "sent", ne)
            op("send%ss.%d" % (s, t), "G", scales, [v(qs, a, e)], [], "sent", ne)
            op("arr%s.%d" % (s, t), "", None, [], [v(qc, C + a, C + e), v(qs, C + a, C + e)], sem, 2 * ne)

        def layer(ghosts):
            for i, (c, a, e) in enumerate(cuts(*CFG["h"][t], end=C + far)):
                if (a >= C) == ghosts:
                    for b in range(4):
                        s = bank(CFG["l"][i][b], e - a)
                        mm("l%s%d.%d" % (c, b, t), s, v("wq", 128 * b, 128 * b + 128), v("wsc", 128 * b, 128 * b + 128), v(zq, a, e), v(zs, a, e))
                        move("r%s%d.%d" % (c, b, t), v(h, 4 * a + b, 4 * e, 4), s, relu=0.015625)
                    quant("h%s.%d" % (c, t), v(hq, a, e), v(hs, a, e), v(h, 4 * a, 4 * e))

        def unpack(ghosts):
            for i, (c, a, e) in enumerate(cuts(*CFG["m"][t], end=W)):
                if (e > C) == ghosts:
                    for b in range(4):
                        s = bank(CFG["mb"][i][b], e - a)
                        mm("m%s%d.%d" % (c, b, t), s, v("eq", 128 * b, 128 * b + 128), v("es", 128 * b, 128 * b + 128), v(hq, a, e), v(hs, a, e))
                        move("d%s%d.%d" % (c, b, t), v(nxt, 4 * a + b, 4 * e, 4), s)

        if far:
            send("F", zq, zs, 0, far)
        for i, (c, a, e) in enumerate(parts("sc")):
            mm("ms%s.%d" % (c, t), bank(CFG["ms"][i], e - a), v("uq2"), v("us2"), v(zq, a, e), v(zs, a, e))
            move("sc%s.%d" % (c, t), v("sc", a, e), bank(CFG["ms"][i], e - a))
        layer(False)
        if far < G:
            send("H", hq, hs, far, G)
        for c, a, e in parts("og"):
            move("og%s.%d" % (c, t), v("og", a, e), v("sc"), v("lh16", k + a // 16, k + e // 16))
        for c, a, e in parts("dd"):
            tt("dd%s.%d" % (c, t), v("sw", a, e), v("sc"), v("og", a, e), A.is_gt, v("lh16", R * K + k + a // 16, R * K + k + e // 16))
        scan("t1.%d" % t, v("t1", 0, 3 * C, 3), v("c16"), v("sw"))
        scan("e1.%d" % t, v("ee"), v("ed", 3 * k, 3 * (k + K)), v("t1", 45, 3 * C + 30, 16), 0.0, A.mult, A.add)
        move("so.%d" % t, v("so"), v("ee", 2, 3 * K, 3), on="V")
        for c, a, e in parts("gsig"):
            move("gsig%s.%d" % (c, t), v("sig", a, e), v("low"), v("so", a // 16, e // 16))
        move("gnx.%d" % t, v("nxh" if CFG.get("n16") else "nxf%d" % (t + 1)), v("nxf%d" % t, 0, C), v("so"))
        for c, a, e in parts("gpv"):
            move("gpv%s.%d" % (c, t), v("pvh", a, e), v("sig"), v("po%d" % t, a // 16, e // 16))
        if CFG.get("n16"):
            scan("scn.%d" % t, v("sn"), v("c4"), v("nxh"), DROP)
            ts("nq.%d" % t, v("nq%d" % (t + 1)), v("sn", 3, C, 4), 4.0, A.mult, col(4), A.add)
            act("nc.%d" % (t + 1), v("nxf%d" % (t + 1)), v("nxh"), F.Identity, 1.0, LOW if t + 1 == R else 0.0)
        else:
            scan("scn.%d" % t, v("scn"), v("c4"), v("nxf%d" % (t + 1)))
            ts("nq.%d" % t, v("nq%d" % (t + 1)), v("scn", 3, C, 4), 4.0, A.mult, col(3), A.add)
        scan("s4.%d" % t, v("s4"), v("c4"), v("pvh"), DROP)
        ts("pq.%d" % t, v("pq%d" % (t + 1)), v("s4", 3, C, 4), 4.0, A.mult, col(4), A.add)
        if t + 1 < R:
            scan("s16.%d" % t, v("s16"), v("c16"), v("pvh"), DROP)
            ts("po.%d" % t, v("po%d" % (t + 1)), v("s16", 15, C, 16), col(5), A.subtract, LOW, A.add)
        layer(True)
        unpack(False)
        unpack(True)
    store("st_nlo", T.nl[:, 0:C], T["nxf%d" % R][0:128:16, :], v("nxf%d" % R))
    for (c, a, e), b in zip(ch, (6, 7, 5)):
        mm("my" + c, bank(b, e - a), v("vq"), v("vs"), v(zq, a, e), v(zs, a, e))
        move("y" + c, v("yt", a, e), bank(b, e - a))
        store("st_oc" + c, T.oc[:, 4 * a:4 * e], ap(v(zq, a, e)).bitcast(dt.uint8), v(zq, a, e))
        store("st_y" + c, T.y[:, a:e], ap(v("yt", a, e)), v("yt", a, e))
    for i in range(4):
        store("st_os%d" % i, T.osc[4 * i:4 * i + 4, :], T[zs][32 * i:32 * i + 4, 0:C], v(zs, 0, C))
    return ops


def needs(ops):
    names, need = list(ops), {}
    for i, n in enumerate(names):
        rd, wr = ops[n][1], ops[n][2]
        need[n] = [m for m in names[:i]
                   if any(meets(a, b) for a in ops[m][2] for b in rd + wr) or any(meets(a, b) for a in ops[m][1] for b in wr)
                   or any(a[0].startswith("ps") and meets(a, b) for a in ops[m][1] for b in rd)]
    return need


def rank_program(g, core, T, topo):
    if T.rank_of(core) is None:
        return
    order = plan()
    where = {n: q for q in order for n in order[q]}
    ops = build(core, T, topo, where)
    assert sorted(n for n in ops if ops[n][0]) == sorted(where) and all(where[n] in ops[n][5] for n in where)
    need = needs(ops)
    mark, count = {}, {}
    for q in order:
        for n in order[q]:
            s = ops[n][3] or "c" + q
            count[s] = count.get(s, 0) + ops[n][4]
            mark[n] = (s, count[s])
    known = {q: {} for q in order}
    after = {}
    for n in ops:
        if not ops[n][0]:
            mark[n] = (ops[n][3], ops[n][4])
            count[ops[n][3]] = ops[n][4]
            after[n] = {ops[n][3]: ops[n][4]}
    queues = {"V": g.vector, "S": g.scalar, "P": g.tensor, "G": g, "Y": g.sync}
    at = {q: 0 for q in order}
    while any(at[q] < len(order[q]) for q in order):
        ready = [q for q in order if at[q] < len(order[q]) and all(m in after for m in need[order[q][at[q]]])]
        assert ready, [order[q][at[q]] for q in order if at[q] < len(order[q])]
        for q in ready:
            n = order[q][at[q]]
            at[q] += 1
            want = {}
            for m in need[n]:
                s, c = mark[m]
                if c > want.get(s, (0, None))[0]:
                    want[s] = (c, m)
            todo = [s for s in want if want[s][0] > known[q].get(s, 0)]
            for s in todo:
                if not any(o != s and after[want[o][1]].get(s, 0) >= want[s][0] for o in todo):
                    queues[q].wait_ge(T.sem[s], want[s][0])
            for s in todo:
                for o, c in after[want[s][1]].items():
                    known[q][o] = max(known[q].get(o, 0), c)
            ins = ops[n][0](queues[q])
            s, c = mark[n]
            if ins is not None:
                ins.then_inc(T.sem[s], ops[n][4])
            after[n] = dict(known[q])
            after[n][s] = c
    for s in count:
        if count[s] > max(known[q].get(s, 0) for q in order):
            g.wait_ge(T.sem[s], count[s])
